import numpy as np
import ml_dtypes


def mxq(x, axis, fmt="e4m3"):
    dtype, down = {"e4m3": (ml_dtypes.float8_e4m3fn, 7), "e5m2": (ml_dtypes.float8_e5m2, 14)}[fmt]
    v = np.moveaxis(np.asarray(x, np.float32).astype(ml_dtypes.bfloat16).astype(np.float64), axis, -1)
    blocks = v.reshape(v.shape[:-1] + (-1, 32))
    amax = np.abs(blocks).max(-1, keepdims=True)
    byte = np.maximum(np.where(amax > 0, np.frexp(amax)[1] - 1 + 127, 0) - down, 1)
    scale = np.exp2(byte - 127.0)
    codes = (blocks / scale).astype(np.float32).astype(dtype).astype(np.float64)
    return np.moveaxis((codes * scale).reshape(v.shape), -1, axis)


WIDE = False


def mx_kscale(k):
    if not WIDE:
        return np.ones(k)
    levels = np.array([10, -10, 5, -5, 0])
    if k % 512:
        return np.exp2(np.random.permutation(np.resize(levels, k // 32))).repeat(32)
    a = np.empty((k // 512, 16))
    for p in range(k // 512):
        a[p, :8] = np.random.permutation(np.resize(levels, 8))
        for g in range(8):
            far = levels[np.abs(levels - a[p, g]) >= 10]
            a[p, g + 8] = far[np.random.randint(len(far))]
    return np.exp2(a.ravel()).repeat(32)


def f64(x):
    return np.asarray(x).astype(np.float64)


def striped(idx):
    return np.tile(idx.reshape(-1, 16).T, (8, 1)).astype(np.uint16)


def unstriped(offs):
    return offs[:16].T.reshape(-1).astype(np.int64)


def striped8(idx):
    return np.concatenate([x.reshape(-1, 16).T for x in idx]).astype(np.uint16)


def runs(offs, k):
    lists = np.stack([offs[16 * r : 16 * r + 16].T.reshape(-1) for r in range(8)]).astype(np.int64)
    return lists[np.arange(k) % 512 // 64]


def pack_weight(w):
    k, n = w.shape
    w = f64(np.asarray(w, np.float32).astype(ml_dtypes.bfloat16)).reshape(k // 32, 32, n)
    amax = np.abs(w).max(1)
    byte = np.clip(np.where(amax > 0, np.frexp(amax)[1] - 1 + 127 - 7, 1), 1, 254)
    scaled = (w * np.exp2(127.0 - byte)[:, None, :]).reshape(k, n).astype(np.float32)
    words = np.ascontiguousarray(scaled.reshape(k // 512, 128, 4, n).transpose(0, 1, 3, 2)).astype(ml_dtypes.float8_e4m3fn).view(np.uint8)
    return words, np.ascontiguousarray(byte.astype(np.uint8).reshape(k // 512, 16, n))


def unpack_weight(words, scales):
    g, p, n, _ = words.shape
    vals = np.ascontiguousarray(words).view(ml_dtypes.float8_e4m3fn).astype(np.float64) * np.repeat(np.exp2(scales.astype(np.float64) - 127.0), 8, axis=1)[..., None]
    return vals.transpose(0, 1, 3, 2).reshape(g * 512, n)


K, T, S, V, N, H = 512, 2048, 512, 512, 512, 512


def setup_inputs():
    n = np.random.standard_normal
    s = mx_kscale(K)[:, None]
    u = mx_kscale(H)
    packed_xT = pack_weight(n((K, T)) * s)
    return {
        "x_words": packed_xT[0],
        "x_scales": packed_xT[1],
        "w1": (n((K, H)) / np.sqrt(K) / s * u).astype(np.float32),
        "w2": (n((K, H)) / np.sqrt(K) / s * u).astype(np.float32),
        "w3": (n((H, N)) / np.sqrt(2 * H) / u[:, None]).astype(np.float32),
        "w4": (n((H, N)) / np.sqrt(2 * H) / u[:, None]).astype(np.float32),
        "offs": striped(np.random.permutation(T)[:S]),
        "book": striped(np.random.permutation(T)[:V]),
        "c1": striped8(np.random.randint(0, V, (8, S))),
        "c2": striped8(np.random.randint(0, V, (8, S))),
    }


def reference(x_words, x_scales, w1, w2, w3, w4, offs, book, c1, c2):
    xq = unpack_weight(x_words, x_scales)[:, unstriped(offs)]
    y = mxq(f64(w1), 0, "e4m3").T @ xq
    x_book = unpack_weight(x_words, x_scales)[:, unstriped(book)]
    c = mxq(f64(w2), 0, "e4m3").T @ x_book
    r1 = y - (c[np.arange(H)[:, None], runs(c1, H)])
    z = r1 - (0.5 * (c[np.arange(H)[:, None], runs(c2, H)]))
    return mxq(f64(w3), 0, "e4m3").T @ mxq(r1, 0, "e4m3") + mxq(f64(w4), 0, "e4m3").T @ mxq(z, 0, "e4m3")

@@ -1,0 +1,178 @@
+from contextlib import ExitStack
+
+import concourse.mybir as mybir
+
+K, T, S, V, N, H = 512, 2048, 512, 512, 512, 512
+FLOPS = 2 * K * H * S + 2 * K * H * V + 2 * 2 * H * N * S
+
+F32 = mybir.dt.float32
+BF16 = mybir.dt.bfloat16
+I32 = mybir.dt.int32
+U32 = mybir.dt.uint32
+U16 = mybir.dt.uint16
+U8 = mybir.dt.uint8
+FP8X4 = mybir.dt.float8_e4m3fn_x4
+ADD = mybir.AluOpType.add
+MULT = mybir.AluOpType.mult
+
+P = 128
+PACK = 4
+HALF = 256
+W2_VECTOR_SHARE = 88
+
+
+def tile_picked_rvqres_none_p_kernel(
+    tc, x_words, x_scales, w1, w2, w3, w4, offs, book, c1, c2, out
+):
+    nc = tc.nc
+    with ExitStack() as ctx:
+        lists = ctx.enter_context(tc.tile_pool(name="lists", bufs=1))
+        keep = ctx.enter_context(tc.tile_pool(name="keep", bufs=1))
+        psum = ctx.enter_context(tc.psum_pool(name="psum", bufs=1))
+
+        def load_list(src, name):
+            tile = lists.tile([P, S // 16], U16, name=name)
+            nc.sync.dma_start(tile[:], src)
+            return tile
+
+        def load_weight(w, name):
+            raw = keep.tile([P, PACK, w.shape[1]], F32, name=name)
+            nc.sync.dma_start(raw[:], w.rearrange("(p j) n -> p j n", j=PACK))
+            return raw
+
+        def operand(name, width):
+            codes = keep.tile([P, width], U32, name=name + "_codes", align_bytes=64)
+            scales = keep.tile([P, width], U8, name=name + "_scales", align_bytes=64)
+            return codes, scales
+
+        def quantize(grouped, name):
+            codes, scales = operand(name, grouped.shape[1] // PACK)
+            nc.vector.quantize_mx(out=codes[:].bitcast(FP8X4), scales=scales[:], in_=grouped[:])
+            return codes, scales
+
+        def product(acc, left, cols, right, start, stop):
+            nc.tensor.matmul_mx(
+                out=acc,
+                lhsT=left[0][:, cols].bitcast(FP8X4),
+                lhsT_scale=left[1][:, cols],
+                rhs=right[0][:].bitcast(FP8X4),
+                rhs_scale=right[1][:],
+                start=start,
+                stop=stop,
+            )
+
+        def dealt_views(grouped, raw):
+            return (
+                grouped[:].rearrange("p (t m j) -> p m j t", t=PACK, j=PACK),
+                raw[:].rearrange("p j (m t) -> p m j t", t=PACK),
+            )
+
+        def woven_views(grouped, planes, run):
+            return (
+                grouped[:].rearrange("p (c i t) -> p c t i", t=PACK, i=run),
+                planes[:].rearrange("p t (c i) -> p c t i", i=run),
+            )
+
+        def bank(b):
+            return psum.tile([P, 512], F32, name="bank%d" % b)
+
+        x_bytes = keep.tile([P, T], U8, name="x_bytes", align_bytes=64)
+        nc.vector.memset(x_bytes[:].bitcast(I32), 0)
+        book_t = load_list(book, "book_t")
+        offs_t = load_list(offs, "offs_t")
+        for q in range(4):
+            nc.sync.dma_start(
+                x_bytes[32 * q : 32 * q + 4, :].bitcast(I32),
+                x_scales[0, 4 * q : 4 * q + 4, :].bitcast(I32),
+            )
+        w2_raw = load_weight(w2, "w2_raw")
+        x_table = keep.tile([P, T], I32, name="x_table", align_bytes=64)
+        nc.sync.dma_start(x_table[:], x_words[0].rearrange("p n t -> p (n t)").bitcast(I32))
+        c2_t = load_list(c2, "c2_t")
+        w1_raw = load_weight(w1, "w1_raw")
+        c1_t = load_list(c1, "c1_t")
+        w3_raw = load_weight(w3, "w3_raw")
+        w4_raw = load_weight(w4, "w4_raw")
+
+        x_book = operand("x_book", V)
+        x_pick = operand("x_pick", S)
+        nc.vector.tensor_copy(x_book[1][:], x_bytes[:].indirect(book_t[:]))
+        nc.vector.tensor_copy(x_pick[1][:], x_bytes[:].indirect(offs_t[:]))
+
+        w2_g = keep.tile([P, PACK * H], BF16, name="w2_g", align_bytes=64)
+        dst, src = dealt_views(w2_g, w2_raw)
+        nc.vector.tensor_copy(dst[:, :W2_VECTOR_SHARE], src[:, :W2_VECTOR_SHARE])
+        nc.scalar.copy(dst[:, W2_VECTOR_SHARE:], src[:, W2_VECTOR_SHARE:])
+        w2_q = quantize(w2_g, "w2")
+
+        nc.vector.tensor_copy(x_book[0][:], x_table[:].bitcast(U32).indirect(book_t[:]))
+        nc.vector.tensor_copy(x_pick[0][:], x_table[:].bitcast(U32).indirect(offs_t[:]))
+
+        neg_c = []
+        for t in range(PACK):
+            acc = bank(t)
+            product(acc[:], w2_q, slice(P * t, P * (t + 1)), x_book, True, True)
+            plane = keep.tile([P, V], F32, name="neg_c%d" % t)
+            nc.scalar.mul(plane[:], acc[:], -1.0)
+            neg_c.append(plane)
+
+        w1_g = keep.tile([P, PACK * H], BF16, name="w1_g", align_bytes=64)
+        dst, src = dealt_views(w1_g, w1_raw)
+        nc.scalar.copy(dst, src)
+
+        halves = [slice(a * HALF // 16, (a + 1) * HALF // 16) for a in range(2)]
+        second = [keep.tile([P, PACK, HALF], F32, name="second%d" % a) for a in range(2)]
+        for t in range(PACK):
+            for a in range(2):
+                nc.vector.tensor_scalar(
+                    second[a][:, t, :], neg_c[t][:].indirect(c2_t[:, halves[a]]), 0.5, 0.0, MULT, ADD
+                )
+
+        w1_q = quantize(w1_g, "w1")
+        y = keep.tile([P, PACK, S], F32, name="y")
+        for t in range(PACK):
+            acc = bank(PACK + t)
+            product(acc[:], w1_q, slice(P * t, P * (t + 1)), x_pick, True, True)
+            nc.scalar.copy(y[:, t, :], acc[:])
+
+        w3_g = keep.tile([P, PACK * N], BF16, name="w3_g", align_bytes=64)
+        dst, src = woven_views(w3_g, w3_raw, 4)
+        nc.vector.tensor_copy(dst, src)
+        w4_g = keep.tile([P, PACK * N], BF16, name="w4_g", align_bytes=64)
+        dst, src = woven_views(w4_g, w4_raw, 4)
+        nc.scalar.copy(dst, src)
+        w3_q = quantize(w3_g, "w3")
+
+        r1_g, z_g = [], []
+        for a in range(2):
+            r1 = keep.tile([P, PACK, HALF], F32, name="r1_%d" % a)
+            for t in range(PACK):
+                nc.vector.tensor_tensor(
+                    r1[:, t, :],
+                    neg_c[t][:].indirect(c1_t[:, halves[a]]),
+                    y[:, t, a * HALF : (a + 1) * HALF],
+                    ADD,
+                )
+            r1_g.append(keep.tile([P, PACK * HALF], BF16, name="r1_g%d" % a, align_bytes=64))
+            dst, src = woven_views(r1_g[a], r1, 4)
+            nc.scalar.copy(dst, src)
+            z_g.append(keep.tile([P, PACK * HALF], BF16, name="z_g%d" % a, align_bytes=64))
+            dst, src = woven_views(z_g[a], r1, 2)
+            nc.vector.tensor_tensor(dst, src, woven_views(z_g[a], second[a], 2)[1], ADD)
+            if a == 0:
+                w4_q = quantize(w4_g, "w4")
+            r1_q = quantize(r1_g[a], "r1_%d" % a)
+            z_q = quantize(z_g[a], "z_%d" % a)
+            staged = keep.tile([P, PACK, HALF], F32, name="staged%d" % a)
+            for m in range(PACK):
+                acc = bank(PACK * a + m)
+                cols = slice(P * m, P * (m + 1))
+                product(acc[:, :HALF], w3_q, cols, r1_q, True, False)
+                product(acc[:, :HALF], w4_q, cols, z_q, False, True)
+                if a == 1 and m % 2 == 1:
+                    nc.vector.tensor_copy(staged[:, m, :], acc[:, :HALF])
+                else:
+                    nc.scalar.copy(staged[:, m, :], acc[:, :HALF])
+            view = out[:, a * HALF : (a + 1) * HALF].rearrange("(m p) j -> p m j", p=P)
+            for s in range(2):
+                nc.sync.dma_start(view[:, 2 * s : 2 * s + 2, :], staged[:, 2 * s : 2 * s + 2, :])

@@ -18,7 +18,6 @@ MULT = mybir.AluOpType.mult
 P = 128
 PACK = 4
 HALF = 256
-W2_VECTOR_SHARE = 88
 
 
 def tile_picked_rvqres_none_p_kernel(
@@ -40,6 +39,11 @@ def tile_picked_rvqres_none_p_kernel(
             nc.sync.dma_start(raw[:], w.rearrange("(p j) n -> p j n", j=PACK))
             return raw
 
+        def load_weight_half(w, h, name):
+            raw = keep.tile([P, PACK, HALF], F32, name=name)
+            nc.sync.dma_start(raw[:], w[:, h * HALF : (h + 1) * HALF].rearrange("(p j) n -> p j n", j=PACK))
+            return raw
+
         def operand(name, width):
             codes = keep.tile([P, width], U32, name=name + "_codes", align_bytes=64)
             scales = keep.tile([P, width], U8, name=name + "_scales", align_bytes=64)
@@ -47,7 +51,7 @@ def tile_picked_rvqres_none_p_kernel(
 
         def quantize(grouped, name):
             codes, scales = operand(name, grouped.shape[1] // PACK)
-            nc.vector.quantize_mx(out=codes[:].bitcast(FP8X4), scales=scales[:], in_=grouped[:])
+            nc.vector.quantize_mx(out=codes[:].bitcast(FP8X4), scales=scales[:], in_=grouped)
             return codes, scales
 
         def product(acc, left, cols, right, start, stop):
@@ -61,35 +65,36 @@ def tile_picked_rvqres_none_p_kernel(
                 stop=stop,
             )
 
-        def dealt_views(grouped, raw):
+        def dealt_views(grouped, raw, h):
             return (
-                grouped[:].rearrange("p (t m j) -> p m j t", t=PACK, j=PACK),
+                grouped[:].rearrange("p (t m j) -> p m j t", t=PACK, j=PACK)[:, 64 * h : 64 * (h + 1)],
                 raw[:].rearrange("p j (m t) -> p m j t", t=PACK),
             )
 
         def woven_views(grouped, planes, run):
             return (
-                grouped[:].rearrange("p (c i t) -> p c t i", t=PACK, i=run),
-                planes[:].rearrange("p t (c i) -> p c t i", i=run),
+                grouped.rearrange("p (c i t) -> p c t i", t=PACK, i=run),
+                planes.rearrange("p t (c i) -> p c t i", i=run),
             )
 
         def bank(b):
             return psum.tile([P, 512], F32, name="bank%d" % b)
 
         x_bytes = keep.tile([P, T], U8, name="x_bytes", align_bytes=64)
-        nc.vector.memset(x_bytes[:].bitcast(I32), 0)
+        nc.vector.memset(x_bytes[:, : T // 2].bitcast(I32), 0)
+        nc.gpsimd.memset(x_bytes[:, T // 2 :].bitcast(I32), 0)
         book_t = load_list(book, "book_t")
         offs_t = load_list(offs, "offs_t")
+        c2_t = load_list(c2, "c2_t")
         for q in range(4):
             nc.sync.dma_start(
                 x_bytes[32 * q : 32 * q + 4, :].bitcast(I32),
                 x_scales[0, 4 * q : 4 * q + 4, :].bitcast(I32),
             )
-        w2_raw = load_weight(w2, "w2_raw")
         x_table = keep.tile([P, T], I32, name="x_table", align_bytes=64)
         nc.sync.dma_start(x_table[:], x_words[0].rearrange("p n t -> p (n t)").bitcast(I32))
-        c2_t = load_list(c2, "c2_t")
-        w1_raw = load_weight(w1, "w1_raw")
+        w2_raw = [load_weight_half(w2, h, "w2_raw%d" % h) for h in range(2)]
+        w1_raw = [load_weight_half(w1, h, "w1_raw%d" % h) for h in range(2)]
         c1_t = load_list(c1, "c1_t")
         w3_raw = load_weight(w3, "w3_raw")
         w4_raw = load_weight(w4, "w4_raw")
@@ -98,37 +103,32 @@ def tile_picked_rvqres_none_p_kernel(
         x_pick = operand("x_pick", S)
         nc.vector.tensor_copy(x_book[1][:], x_bytes[:].indirect(book_t[:]))
         nc.vector.tensor_copy(x_pick[1][:], x_bytes[:].indirect(offs_t[:]))
-
-        w2_g = keep.tile([P, PACK * H], BF16, name="w2_g", align_bytes=64)
-        dst, src = dealt_views(w2_g, w2_raw)
-        nc.vector.tensor_copy(dst[:, :W2_VECTOR_SHARE], src[:, :W2_VECTOR_SHARE])
-        nc.scalar.copy(dst[:, W2_VECTOR_SHARE:], src[:, W2_VECTOR_SHARE:])
-        w2_q = quantize(w2_g, "w2")
-
         nc.vector.tensor_copy(x_book[0][:], x_table[:].bitcast(U32).indirect(book_t[:]))
         nc.vector.tensor_copy(x_pick[0][:], x_table[:].bitcast(U32).indirect(offs_t[:]))
+
+        w2_g = keep.tile([P, PACK * H], BF16, name="w2_g", align_bytes=64)
+        nc.scalar.copy(*dealt_views(w2_g, w2_raw[0], 0))
+        nc.vector.tensor_copy(*dealt_views(w2_g, w2_raw[1], 1))
+        w2_q = quantize(w2_g[:], "w2")
+
+        w1_g = keep.tile([P, PACK * H], BF16, name="w1_g", align_bytes=64)
+        nc.scalar.copy(*dealt_views(w1_g, w1_raw[0], 0))
+        nc.vector.tensor_copy(*dealt_views(w1_g, w1_raw[1], 1))
+        w1_q = quantize(w1_g[:], "w1")
 
         neg_c = []
         for t in range(PACK):
             acc = bank(t)
             product(acc[:], w2_q, slice(P * t, P * (t + 1)), x_book, True, True)
-            plane = keep.tile([P, V], F32, name="neg_c%d" % t)
-            nc.scalar.mul(plane[:], acc[:], -1.0)
+            plane = keep.tile([P, 2 * V], F32, name="neg_c%d" % t)
+            nc.scalar.mul(plane[:, :V], acc[:], -1.0)
             neg_c.append(plane)
 
-        w1_g = keep.tile([P, PACK * H], BF16, name="w1_g", align_bytes=64)
-        dst, src = dealt_views(w1_g, w1_raw)
-        nc.scalar.copy(dst, src)
-
         halves = [slice(a * HALF // 16, (a + 1) * HALF // 16) for a in range(2)]
-        second = [keep.tile([P, PACK, HALF], F32, name="second%d" % a) for a in range(2)]
+        second = keep.tile([P, PACK, S], F32, name="second")
         for t in range(PACK):
-            for a in range(2):
-                nc.vector.tensor_scalar(
-                    second[a][:, t, :], neg_c[t][:].indirect(c2_t[:, halves[a]]), 0.5, 0.0, MULT, ADD
-                )
+            nc.vector.tensor_scalar(second[:, t, :], neg_c[t][:].indirect(c2_t[:]), 0.5, 0.0, MULT, ADD)
 
-        w1_q = quantize(w1_g, "w1")
         y = keep.tile([P, PACK, S], F32, name="y")
         for t in range(PACK):
             acc = bank(PACK + t)
@@ -136,43 +136,42 @@ def tile_picked_rvqres_none_p_kernel(
             nc.scalar.copy(y[:, t, :], acc[:])
 
         w3_g = keep.tile([P, PACK * N], BF16, name="w3_g", align_bytes=64)
-        dst, src = woven_views(w3_g, w3_raw, 4)
-        nc.vector.tensor_copy(dst, src)
+        nc.scalar.copy(*woven_views(w3_g[:], w3_raw[:], 4))
         w4_g = keep.tile([P, PACK * N], BF16, name="w4_g", align_bytes=64)
-        dst, src = woven_views(w4_g, w4_raw, 4)
-        nc.scalar.copy(dst, src)
-        w3_q = quantize(w3_g, "w3")
+        nc.scalar.copy(*woven_views(w4_g[:], w4_raw[:], 4))
 
-        r1_g, z_g = [], []
+        r1 = [keep.tile([P, PACK, HALF], F32, name="r1_%d" % a, align_bytes=64) for a in range(2)]
+        reused = r1[1][:].rearrange("p t j -> p (t j)").bitcast(BF16)
+        z_g = [reused[:, : PACK * HALF], keep.tile([P, PACK * HALF], BF16, name="z_g1", align_bytes=64)[:]]
+        r1_g = [reused[:, PACK * HALF :], keep.tile([P, PACK * HALF], BF16, name="r1_g1", align_bytes=64)[:]]
         for a in range(2):
-            r1 = keep.tile([P, PACK, HALF], F32, name="r1_%d" % a)
             for t in range(PACK):
                 nc.vector.tensor_tensor(
-                    r1[:, t, :],
+                    r1[a][:, t, :],
                     neg_c[t][:].indirect(c1_t[:, halves[a]]),
                     y[:, t, a * HALF : (a + 1) * HALF],
                     ADD,
                 )
-            r1_g.append(keep.tile([P, PACK * HALF], BF16, name="r1_g%d" % a, align_bytes=64))
-            dst, src = woven_views(r1_g[a], r1, 4)
-            nc.scalar.copy(dst, src)
-            z_g.append(keep.tile([P, PACK * HALF], BF16, name="z_g%d" % a, align_bytes=64))
-            dst, src = woven_views(z_g[a], r1, 2)
-            nc.vector.tensor_tensor(dst, src, woven_views(z_g[a], second[a], 2)[1], ADD)
-            if a == 0:
-                w4_q = quantize(w4_g, "w4")
-            r1_q = quantize(r1_g[a], "r1_%d" % a)
+            nc.scalar.copy(*woven_views(r1_g[a], r1[a][:], 4))
+            dst, src = woven_views(z_g[a], r1[a][:], 2)
+            nc.vector.tensor_tensor(dst, src, woven_views(z_g[a], second[:, :, a * HALF : (a + 1) * HALF], 2)[1], ADD)
             z_q = quantize(z_g[a], "z_%d" % a)
+            if a == 0:
+                w3_q = quantize(w3_g[:], "w3")
+                w4_q = quantize(w4_g[:], "w4")
+            r1_q = quantize(r1_g[a], "r1_%d" % a)
             staged = keep.tile([P, PACK, HALF], F32, name="staged%d" % a)
+            accs = [bank(PACK * a + m) for m in range(PACK)]
             for m in range(PACK):
-                acc = bank(PACK * a + m)
-                cols = slice(P * m, P * (m + 1))
-                product(acc[:, :HALF], w3_q, cols, r1_q, True, False)
-                product(acc[:, :HALF], w4_q, cols, z_q, False, True)
-                if a == 1 and m % 2 == 1:
-                    nc.vector.tensor_copy(staged[:, m, :], acc[:, :HALF])
-                else:
-                    nc.scalar.copy(staged[:, m, :], acc[:, :HALF])
+                product(accs[m][:, :HALF], w4_q, slice(P * m, P * (m + 1)), z_q, True, False)
             view = out[:, a * HALF : (a + 1) * HALF].rearrange("(m p) j -> p m j", p=P)
-            for s in range(2):
-                nc.sync.dma_start(view[:, 2 * s : 2 * s + 2, :], staged[:, 2 * s : 2 * s + 2, :])
+            for m in range(PACK):
+                product(accs[m][:, :HALF], w3_q, slice(P * m, P * (m + 1)), r1_q, False, True)
+                if a == 1 and m % 2 == 1:
+                    nc.vector.tensor_copy(staged[:, m, :], accs[m][:, :HALF])
+                else:
+                    nc.scalar.copy(staged[:, m, :], accs[m][:, :HALF])
+                if a == 1:
+                    nc.sync.dma_start(view[:, m, :], staged[:, m, :])
+            if a == 0:
+                nc.sync.dma_start(view, staged[:])

@@ -39,13 +39,8 @@ def tile_picked_rvqres_none_p_kernel(
             nc.sync.dma_start(raw[:], w.rearrange("(p j) n -> p j n", j=PACK))
             return raw
 
-        def load_weight_half(w, h, name):
-            raw = keep.tile([P, PACK, HALF], F32, name=name)
-            nc.sync.dma_start(raw[:], w[:, h * HALF : (h + 1) * HALF].rearrange("(p j) n -> p j n", j=PACK))
-            return raw
-
         def operand(name, width):
-            codes = keep.tile([P, width], U32, name=name + "_codes", align_bytes=64)
+            codes = keep.tile([P, width], U32, name=name + "_codes", tag=name + "_codes", align_bytes=64)
             scales = keep.tile([P, width], U8, name=name + "_scales", align_bytes=64)
             return codes, scales
 
@@ -54,21 +49,21 @@ def tile_picked_rvqres_none_p_kernel(
             nc.vector.quantize_mx(out=codes[:].bitcast(FP8X4), scales=scales[:], in_=grouped)
             return codes, scales
 
-        def product(acc, left, cols, right, start, stop):
+        def product(acc, left, cols, right, right_cols, start, stop):
             nc.tensor.matmul_mx(
                 out=acc,
                 lhsT=left[0][:, cols].bitcast(FP8X4),
                 lhsT_scale=left[1][:, cols],
-                rhs=right[0][:].bitcast(FP8X4),
-                rhs_scale=right[1][:],
+                rhs=right[0][:, right_cols].bitcast(FP8X4),
+                rhs_scale=right[1][:, right_cols],
                 start=start,
                 stop=stop,
             )
 
-        def dealt_views(grouped, raw, h):
+        def dealt_views(grouped, raw, u):
             return (
-                grouped[:].rearrange("p (t m j) -> p m j t", t=PACK, j=PACK)[:, 64 * h : 64 * (h + 1)],
-                raw[:].rearrange("p j (m t) -> p m j t", t=PACK),
+                grouped[:].rearrange("p (t m j) -> p m j t", t=2, j=PACK),
+                raw[:].rearrange("p j (m t) -> p m j t", t=PACK)[:, :, :, 2 * u : 2 * u + 2],
             )
 
         def woven_views(grouped, planes, run):
@@ -81,8 +76,7 @@ def tile_picked_rvqres_none_p_kernel(
             return psum.tile([P, 512], F32, name="bank%d" % b)
 
         x_bytes = keep.tile([P, T], U8, name="x_bytes", align_bytes=64)
-        nc.vector.memset(x_bytes[:, : T // 2].bitcast(I32), 0)
-        nc.gpsimd.memset(x_bytes[:, T // 2 :].bitcast(I32), 0)
+        nc.vector.memset(x_bytes[:].bitcast(I32), 0)
         book_t = load_list(book, "book_t")
         offs_t = load_list(offs, "offs_t")
         c2_t = load_list(c2, "c2_t")
@@ -93,11 +87,14 @@ def tile_picked_rvqres_none_p_kernel(
             )
         x_table = keep.tile([P, T], I32, name="x_table", align_bytes=64)
         nc.sync.dma_start(x_table[:], x_words[0].rearrange("p n t -> p (n t)").bitcast(I32))
-        w2_raw = [load_weight_half(w2, h, "w2_raw%d" % h) for h in range(2)]
-        w1_raw = [load_weight_half(w1, h, "w1_raw%d" % h) for h in range(2)]
+        w2_raw = load_weight(w2, "w2_raw")
+        w1_raw = load_weight(w1, "w1_raw")
         c1_t = load_list(c1, "c1_t")
         w3_raw = load_weight(w3, "w3_raw")
         w4_raw = load_weight(w4, "w4_raw")
+
+        def pair_tile(name, tag):
+            return keep.tile([P, 2 * H], BF16, name=name, tag=tag, align_bytes=64)
 
         x_book = operand("x_book", V)
         x_pick = operand("x_pick", S)
@@ -106,72 +103,82 @@ def tile_picked_rvqres_none_p_kernel(
         nc.vector.tensor_copy(x_book[0][:], x_table[:].bitcast(U32).indirect(book_t[:]))
         nc.vector.tensor_copy(x_pick[0][:], x_table[:].bitcast(U32).indirect(offs_t[:]))
 
-        w2_g = keep.tile([P, PACK * H], BF16, name="w2_g", align_bytes=64)
-        nc.scalar.copy(*dealt_views(w2_g, w2_raw[0], 0))
-        nc.vector.tensor_copy(*dealt_views(w2_g, w2_raw[1], 1))
-        w2_q = quantize(w2_g[:], "w2")
+        w2_g = [pair_tile("w2_g%d" % u, "w2_g%d" % u) for u in range(2)]
+        nc.vector.tensor_copy(*dealt_views(w2_g[0], w2_raw, 0))
+        nc.scalar.copy(*dealt_views(w2_g[1], w2_raw, 1))
+        w2_q = [quantize(w2_g[u][:], "w2_%d" % u) for u in range(2)]
 
-        w1_g = keep.tile([P, PACK * H], BF16, name="w1_g", align_bytes=64)
-        nc.scalar.copy(*dealt_views(w1_g, w1_raw[0], 0))
-        nc.vector.tensor_copy(*dealt_views(w1_g, w1_raw[1], 1))
-        w1_q = quantize(w1_g[:], "w1")
-
-        neg_c = []
+        whole = slice(0, 512)
+        c_acc = [bank(t) for t in range(PACK)]
         for t in range(PACK):
-            acc = bank(t)
-            product(acc[:], w2_q, slice(P * t, P * (t + 1)), x_book, True, True)
-            plane = keep.tile([P, 2 * V], F32, name="neg_c%d" % t)
-            nc.scalar.mul(plane[:, :V], acc[:], -1.0)
-            neg_c.append(plane)
-
-        halves = [slice(a * HALF // 16, (a + 1) * HALF // 16) for a in range(2)]
+            product(c_acc[t][:], w2_q[t // 2], slice(P * (t % 2), P * (t % 2 + 1)), x_book, whole, True, True)
+        neg_c = [keep.tile([P, 2 * V], F32, name="neg_c%d" % t) for t in range(PACK)]
         second = keep.tile([P, PACK, S], F32, name="second")
-        for t in range(PACK):
+
+        def look_up_second(t):
+            nc.scalar.mul(neg_c[t][:, :V], c_acc[t][:], -1.0)
             nc.vector.tensor_scalar(second[:, t, :], neg_c[t][:].indirect(c2_t[:]), 0.5, 0.0, MULT, ADD)
+
+        w1_g = [pair_tile("w1_g0", "w2_g1"), pair_tile("w1_g1", "w2_0_codes")]
+        nc.vector.tensor_copy(*dealt_views(w1_g[0], w1_raw, 0))
+        w1_q = [quantize(w1_g[0][:], "w1_0")]
+        look_up_second(0)
+        nc.scalar.copy(*dealt_views(w1_g[1], w1_raw, 1))
+        w1_q.append(quantize(w1_g[1][:], "w1_1"))
+        for t in range(1, PACK):
+            look_up_second(t)
 
         y = keep.tile([P, PACK, S], F32, name="y")
         for t in range(PACK):
             acc = bank(PACK + t)
-            product(acc[:], w1_q, slice(P * t, P * (t + 1)), x_pick, True, True)
+            product(acc[:], w1_q[t // 2], slice(P * (t % 2), P * (t % 2 + 1)), x_pick, whole, True, True)
             nc.scalar.copy(y[:, t, :], acc[:])
-
         w3_g = keep.tile([P, PACK * N], BF16, name="w3_g", align_bytes=64)
         nc.scalar.copy(*woven_views(w3_g[:], w3_raw[:], 4))
-        w4_g = keep.tile([P, PACK * N], BF16, name="w4_g", align_bytes=64)
+
+        halves = [slice(a * HALF, (a + 1) * HALF) for a in range(2)]
+        narrow = halves[0]
+
+        w4_g = keep.tile([P, PACK * N], BF16, name="w4_g", tag="w4_g", align_bytes=64)
         nc.scalar.copy(*woven_views(w4_g[:], w4_raw[:], 4))
 
-        r1 = [keep.tile([P, PACK, HALF], F32, name="r1_%d" % a, align_bytes=64) for a in range(2)]
-        reused = r1[1][:].rearrange("p t j -> p (t j)").bitcast(BF16)
-        z_g = [reused[:, : PACK * HALF], keep.tile([P, PACK * HALF], BF16, name="z_g1", align_bytes=64)[:]]
-        r1_g = [reused[:, PACK * HALF :], keep.tile([P, PACK * HALF], BF16, name="r1_g1", align_bytes=64)[:]]
+        r1 = keep.tile([P, PACK, S], F32, name="r1")
+        for t in range(PACK):
+            nc.vector.tensor_tensor(r1[:, t, :], neg_c[t][:].indirect(c1_t[:]), y[:, t, :], ADD)
+        r1_g = []
         for a in range(2):
-            for t in range(PACK):
-                nc.vector.tensor_tensor(
-                    r1[a][:, t, :],
-                    neg_c[t][:].indirect(c1_t[:, halves[a]]),
-                    y[:, t, a * HALF : (a + 1) * HALF],
-                    ADD,
-                )
-            nc.scalar.copy(*woven_views(r1_g[a], r1[a][:], 4))
-            dst, src = woven_views(z_g[a], r1[a][:], 2)
-            nc.vector.tensor_tensor(dst, src, woven_views(z_g[a], second[:, :, a * HALF : (a + 1) * HALF], 2)[1], ADD)
-            z_q = quantize(z_g[a], "z_%d" % a)
-            if a == 0:
-                w3_q = quantize(w3_g[:], "w3")
-                w4_q = quantize(w4_g[:], "w4")
-            r1_q = quantize(r1_g[a], "r1_%d" % a)
-            staged = keep.tile([P, PACK, HALF], F32, name="staged%d" % a)
+            r1_g.append(keep.tile([P, PACK * HALF], BF16, name="r1_g%d" % a, tag="r1_g%d" % a, align_bytes=64))
+            nc.scalar.copy(*woven_views(r1_g[a][:], r1[:, :, halves[a]], 4))
+        w3_q = quantize(w3_g[:], "w3")
+        w4_q = quantize(w4_g[:], "w4")
+
+        def second_remainder(a, tag):
+            z_g = keep.tile([P, PACK * HALF], BF16, name="z_g%d" % a, tag=tag, align_bytes=64)
+            dst, src = woven_views(z_g[:], r1[:, :, halves[a]], 2)
+            nc.vector.tensor_tensor(dst, src, woven_views(z_g[:], second[:, :, halves[a]], 2)[1], ADD)
+            return z_g
+
+        def open_groups(a, r1_q):
             accs = [bank(PACK * a + m) for m in range(PACK)]
             for m in range(PACK):
-                product(accs[m][:, :HALF], w4_q, slice(P * m, P * (m + 1)), z_q, True, False)
-            view = out[:, a * HALF : (a + 1) * HALF].rearrange("(m p) j -> p m j", p=P)
+                product(accs[m][:, narrow], w3_q, slice(P * m, P * (m + 1)), r1_q, narrow, True, False)
+            return accs
+
+        def close_groups(a, accs, z_q):
+            staged = keep.tile([P, PACK, HALF], F32, name="staged%d" % a)
+            view = out[:, halves[a]].rearrange("(m p) j -> p m j", p=P)
             for m in range(PACK):
-                product(accs[m][:, :HALF], w3_q, slice(P * m, P * (m + 1)), r1_q, False, True)
+                product(accs[m][:, narrow], w4_q, slice(P * m, P * (m + 1)), z_q, narrow, False, True)
                 if a == 1 and m % 2 == 1:
-                    nc.vector.tensor_copy(staged[:, m, :], accs[m][:, :HALF])
+                    nc.vector.tensor_copy(staged[:, m, :], accs[m][:, narrow])
                 else:
-                    nc.scalar.copy(staged[:, m, :], accs[m][:, :HALF])
+                    nc.scalar.copy(staged[:, m, :], accs[m][:, narrow])
                 if a == 1:
                     nc.sync.dma_start(view[:, m, :], staged[:, m, :])
             if a == 0:
                 nc.sync.dma_start(view, staged[:])
+
+        for a in range(2):
+            z_g = second_remainder(a, ("w4_g", "r1_g0")[a])
+            accs = open_groups(a, quantize(r1_g[a][:], "r1_%d" % a))
+            close_groups(a, accs, quantize(z_g[:], "z_%d" % a))

@@ -150,6 +150,8 @@ def tile_picked_rvqres_none_p_kernel(
             r1_g.append(keep.tile([P, PACK * HALF], BF16, name="r1_g%d" % a, tag="r1_g%d" % a, align_bytes=64))
             nc.scalar.copy(*woven_views(r1_g[a][:], r1[:, :, halves[a]], 4))
         w3_q = quantize(w3_g[:], "w3")
+        for m in range(PACK):
+            product(bank(PACK + m)[:], w3_q, slice(P * m, P * (m + 1)), x_pick, whole, True, True)
         w4_q = quantize(w4_g[:], "w4")
 
         def second_remainder(a, tag):
@@ -173,10 +175,7 @@ def tile_picked_rvqres_none_p_kernel(
                     nc.vector.tensor_copy(staged[:, m, :], accs[m][:, narrow])
                 else:
                     nc.scalar.copy(staged[:, m, :], accs[m][:, narrow])
-                if a == 1:
-                    nc.sync.dma_start(view[:, m, :], staged[:, m, :])
-            if a == 0:
-                nc.sync.dma_start(view, staged[:])
+                nc.sync.dma_start(view[:, m, :], staged[:, m, :])
 
         for a in range(2):
             z_g = second_remainder(a, ("w4_g", "r1_g0")[a])

@@ -18,6 +18,8 @@ MULT = mybir.AluOpType.mult
 P = 128
 PACK = 4
 HALF = 256
+CHUNKS = (slice(0, 256), slice(256, 512))
+SHARE = 80
 
 
 def tile_picked_rvqres_none_p_kernel(
@@ -35,17 +37,17 @@ def tile_picked_rvqres_none_p_kernel(
             return tile
 
         def load_weight(w, name):
-            raw = keep.tile([P, PACK, w.shape[1]], F32, name=name)
+            raw = keep.tile([P, PACK, w.shape[1]], F32, name=name, tag=name, align_bytes=64)
             nc.sync.dma_start(raw[:], w.rearrange("(p j) n -> p j n", j=PACK))
             return raw
 
-        def operand(name, width):
-            codes = keep.tile([P, width], U32, name=name + "_codes", tag=name + "_codes", align_bytes=64)
-            scales = keep.tile([P, width], U8, name=name + "_scales", align_bytes=64)
+        def operand(name, width, tag=None):
+            codes = keep.tile([P, width], U32, name=name + "_codes", tag=tag or name + "_codes", align_bytes=64)
+            scales = keep.tile([P, width], U8, name=name + "_scales", tag=name + "_scales", align_bytes=64)
             return codes, scales
 
-        def quantize(grouped, name):
-            codes, scales = operand(name, grouped.shape[1] // PACK)
+        def quantize(grouped, name, tag=None):
+            codes, scales = operand(name, grouped.shape[1] // PACK, tag)
             nc.vector.quantize_mx(out=codes[:].bitcast(FP8X4), scales=scales[:], in_=grouped)
             return codes, scales
 
@@ -62,7 +64,7 @@ def tile_picked_rvqres_none_p_kernel(
 
         def dealt_views(grouped, raw, u):
             return (
-                grouped[:].rearrange("p (t m j) -> p m j t", t=2, j=PACK),
+                grouped.rearrange("p (t m j) -> p m j t", t=2, j=PACK),
                 raw[:].rearrange("p j (m t) -> p m j t", t=PACK)[:, :, :, 2 * u : 2 * u + 2],
             )
 
@@ -75,6 +77,13 @@ def tile_picked_rvqres_none_p_kernel(
         def bank(b):
             return psum.tile([P, 512], F32, name="bank%d" % b)
 
+        def rows(t):
+            return slice(P * t, P * (t + 1))
+
+        def entries(tile, first, count):
+            return tile[:, first // 16 : (first + count) // 16]
+
+        halves = [slice(h * HALF, (h + 1) * HALF) for h in range(2)]
         x_bytes = keep.tile([P, T], U8, name="x_bytes", align_bytes=64)
         nc.vector.memset(x_bytes[:].bitcast(I32), 0)
         book_t = load_list(book, "book_t")
@@ -97,87 +106,110 @@ def tile_picked_rvqres_none_p_kernel(
             return keep.tile([P, 2 * H], BF16, name=name, tag=tag, align_bytes=64)
 
         x_book = operand("x_book", V)
-        x_pick = operand("x_pick", S)
+        pick_scales = keep.tile([P, S], U8, name="pick_scales", align_bytes=64)
         nc.vector.tensor_copy(x_book[1][:], x_bytes[:].indirect(book_t[:]))
-        nc.vector.tensor_copy(x_pick[1][:], x_bytes[:].indirect(offs_t[:]))
+        nc.vector.tensor_copy(pick_scales[:], x_bytes[:].indirect(offs_t[:]))
         nc.vector.tensor_copy(x_book[0][:], x_table[:].bitcast(U32).indirect(book_t[:]))
-        nc.vector.tensor_copy(x_pick[0][:], x_table[:].bitcast(U32).indirect(offs_t[:]))
+        early_words = keep.tile([P, HALF], U32, name="early_words", align_bytes=64)
+        nc.vector.tensor_copy(early_words[:], x_table[:].bitcast(U32).indirect(entries(offs_t, 0, HALF)))
 
         w2_g = [pair_tile("w2_g%d" % u, "w2_g%d" % u) for u in range(2)]
-        nc.vector.tensor_copy(*dealt_views(w2_g[0], w2_raw, 0))
-        nc.scalar.copy(*dealt_views(w2_g[1], w2_raw, 1))
-        w2_q = [quantize(w2_g[u][:], "w2_%d" % u) for u in range(2)]
+        dst, src = dealt_views(w2_g[0][:], w2_raw, 0)
+        nc.vector.tensor_copy(dst[:, :SHARE], src[:, :SHARE])
+        nc.scalar.copy(dst[:, SHARE:], src[:, SHARE:])
+        nc.scalar.copy(*dealt_views(w2_g[1][:], w2_raw, 1))
+        w2_q = [operand("w2_0", HALF)]
+        for t in range(2):
+            nc.vector.quantize_mx(
+                out=w2_q[0][0][:, rows(t)].bitcast(FP8X4), scales=w2_q[0][1][:, rows(t)], in_=w2_g[0][:, H * t : H * (t + 1)]
+            )
+        late_words = keep.tile([P, HALF], U32, name="late_words", tag="w2_g0", align_bytes=64)
+        nc.vector.tensor_copy(late_words[:], x_table[:].bitcast(U32).indirect(entries(offs_t, HALF, HALF)))
+        x_pick = [(early_words, pick_scales[:, halves[0]]), (late_words, pick_scales[:, halves[1]])]
+        w2_q.append(quantize(w2_g[1][:], "w2_1"))
 
         whole = slice(0, 512)
-        c_acc = [bank(t) for t in range(PACK)]
-        for t in range(PACK):
-            product(c_acc[t][:], w2_q[t // 2], slice(P * (t % 2), P * (t % 2 + 1)), x_book, whole, True, True)
         neg_c = [keep.tile([P, 2 * V], F32, name="neg_c%d" % t) for t in range(PACK)]
+        first_acc = [bank(PACK + h) for h in range(2)]
+        for h in range(2):
+            product(first_acc[h][:, :HALF], w2_q[0], rows(0), x_book, halves[h], True, True)
+            nc.scalar.mul(neg_c[0][:, halves[h]], first_acc[h][:, :HALF], -1.0)
+        c_acc = [None] + [bank(t) for t in range(1, PACK)]
+        for t in range(1, PACK):
+            product(c_acc[t][:], w2_q[t // 2], rows(t % 2), x_book, whole, True, True)
         second = keep.tile([P, PACK, S], F32, name="second")
 
         def look_up_second(t):
-            nc.scalar.mul(neg_c[t][:, :V], c_acc[t][:], -1.0)
+            if t:
+                nc.scalar.mul(neg_c[t][:, :V], c_acc[t][:], -1.0)
             nc.vector.tensor_scalar(second[:, t, :], neg_c[t][:].indirect(c2_t[:]), 0.5, 0.0, MULT, ADD)
 
-        w1_g = [pair_tile("w1_g0", "w2_g1"), pair_tile("w1_g1", "w2_0_codes")]
-        nc.vector.tensor_copy(*dealt_views(w1_g[0], w1_raw, 0))
-        w1_q = [quantize(w1_g[0][:], "w1_0")]
+        w1_g = [pair_tile("w1_g%d" % u, "w2_%d_codes" % u) for u in range(2)]
+        w1_q = []
         look_up_second(0)
-        nc.scalar.copy(*dealt_views(w1_g[1], w1_raw, 1))
-        w1_q.append(quantize(w1_g[1][:], "w1_1"))
-        for t in range(1, PACK):
-            look_up_second(t)
+        for u in range(2):
+            look_up_second(1 + u)
+            nc.scalar.copy(*dealt_views(w1_g[u][:], w1_raw, u))
+            w1_q.append(quantize(w1_g[u][:], "w1_%d" % u))
+        look_up_second(3)
 
+        y_acc = [bank(PACK + t) for t in range(PACK)]
+        for t in range(PACK):
+            for h in range(2):
+                product(y_acc[t][:, halves[h]], w1_q[t // 2], rows(t % 2), x_pick[h], halves[0], True, True)
         y = keep.tile([P, PACK, S], F32, name="y")
-        for t in range(PACK):
-            acc = bank(PACK + t)
-            product(acc[:], w1_q[t // 2], slice(P * (t % 2), P * (t % 2 + 1)), x_pick, whole, True, True)
-            nc.scalar.copy(y[:, t, :], acc[:])
-        w3_g = keep.tile([P, PACK * N], BF16, name="w3_g", align_bytes=64)
-        nc.scalar.copy(*woven_views(w3_g[:], w3_raw[:], 4))
-
-        halves = [slice(a * HALF, (a + 1) * HALF) for a in range(2)]
-        narrow = halves[0]
-
-        w4_g = keep.tile([P, PACK * N], BF16, name="w4_g", tag="w4_g", align_bytes=64)
-        nc.scalar.copy(*woven_views(w4_g[:], w4_raw[:], 4))
-
         r1 = keep.tile([P, PACK, S], F32, name="r1")
-        for t in range(PACK):
-            nc.vector.tensor_tensor(r1[:, t, :], neg_c[t][:].indirect(c1_t[:]), y[:, t, :], ADD)
-        r1_g = []
-        for a in range(2):
-            r1_g.append(keep.tile([P, PACK * HALF], BF16, name="r1_g%d" % a, tag="r1_g%d" % a, align_bytes=64))
-            nc.scalar.copy(*woven_views(r1_g[a][:], r1[:, :, halves[a]], 4))
-        w3_q = quantize(w3_g[:], "w3")
-        for m in range(PACK):
-            product(bank(PACK + m)[:], w3_q, slice(P * m, P * (m + 1)), x_pick, whole, True, True)
-        w4_q = quantize(w4_g[:], "w4")
+
+        def first_remainder(t, cols):
+            nc.scalar.copy(y[:, t, cols], y_acc[t][:, cols])
+            offsets = entries(c1_t, cols.start, cols.stop - cols.start)
+            nc.vector.tensor_tensor(r1[:, t, cols], neg_c[t][:].indirect(offsets), y[:, t, cols], ADD)
+
+        def woven_tile(name, count, tag=None):
+            return keep.tile([P, PACK * count], BF16, name=name, tag=tag or name, align_bytes=64)
+
+        def weave_first(a):
+            cols = CHUNKS[a]
+            r1_g = woven_tile("r1_g%d" % a, cols.stop - cols.start)
+            nc.scalar.copy(*woven_views(r1_g[:], r1[:, :, cols], 4))
+            return r1_g
 
         def second_remainder(a, tag):
-            z_g = keep.tile([P, PACK * HALF], BF16, name="z_g%d" % a, tag=tag, align_bytes=64)
-            dst, src = woven_views(z_g[:], r1[:, :, halves[a]], 2)
-            nc.vector.tensor_tensor(dst, src, woven_views(z_g[:], second[:, :, halves[a]], 2)[1], ADD)
+            cols = CHUNKS[a]
+            z_g = woven_tile("z_g%d" % a, cols.stop - cols.start, tag)
+            dst, src = woven_views(z_g[:], r1[:, :, cols], 2)
+            nc.vector.tensor_tensor(dst, src, woven_views(z_g[:], second[:, :, cols], 2)[1], ADD)
             return z_g
 
-        def open_groups(a, r1_q):
-            accs = [bank(PACK * a + m) for m in range(PACK)]
-            for m in range(PACK):
-                product(accs[m][:, narrow], w3_q, slice(P * m, P * (m + 1)), r1_q, narrow, True, False)
-            return accs
+        def round_weight(raw, name, tag):
+            grouped = woven_tile(name, N, tag)
+            nc.scalar.copy(*woven_views(grouped[:], raw[:], 4))
+            return grouped
 
-        def close_groups(a, accs, z_q):
-            staged = keep.tile([P, PACK, HALF], F32, name="staged%d" % a)
-            view = out[:, halves[a]].rearrange("(m p) j -> p m j", p=P)
+        def finish(a, banks, factors, engines):
+            count = CHUNKS[a].stop - CHUNKS[a].start
+            accs = [bank(b) for b in banks]
+            view = out[:, CHUNKS[a]].rearrange("(m p) j -> p m j", p=P)
+            for opens, (left, right) in zip((True, False), factors):
+                for m in range(PACK):
+                    product(accs[m][:, :count], left, rows(m), right, slice(0, count), opens, not opens)
             for m in range(PACK):
-                product(accs[m][:, narrow], w4_q, slice(P * m, P * (m + 1)), z_q, narrow, False, True)
-                if a == 1 and m % 2 == 1:
-                    nc.vector.tensor_copy(staged[:, m, :], accs[m][:, narrow])
-                else:
-                    nc.scalar.copy(staged[:, m, :], accs[m][:, narrow])
-                nc.sync.dma_start(view[:, m, :], staged[:, m, :])
+                staged = keep.tile([P, count], F32, name="staged%d_%d" % (a, m))
+                engines[m](staged[:], accs[m][:, :count])
+                nc.sync.dma_start(view[:, m, :], staged[:])
 
-        for a in range(2):
-            z_g = second_remainder(a, ("w4_g", "r1_g0")[a])
-            accs = open_groups(a, quantize(r1_g[a][:], "r1_%d" % a))
-            close_groups(a, accs, quantize(z_g[:], "z_%d" % a))
+        for t in range(PACK):
+            first_remainder(t, whole)
+        w3_q = quantize(round_weight(w3_raw, "w3_g", "w1_1_codes")[:], "w3")
+        for m in range(2):
+            product(bank(PACK + m)[:], w3_q, rows(m), x_book, whole, True, True)
+        z_ga = second_remainder(0, "w3_raw")
+        w4_q = quantize(round_weight(w4_raw, "w4_g", "w2_g0")[:], "w4")
+        r1_g = [weave_first(a) for a in range(2)]
+        z_qa = quantize(z_ga[:], "z_0")
+        r1_qa = quantize(r1_g[0][:], "r1_0")
+        finish(0, (0, 1, 2, 3), ((w4_q, z_qa), (w3_q, r1_qa)), [nc.scalar.copy] * PACK)
+        z_gb = second_remainder(1, "r1_g0")
+        r1_qb = quantize(r1_g[1][:], "r1_1")
+        z_qb = quantize(z_gb[:], "z_1")
+        finish(1, (4, 5, 6, 7), ((w3_q, r1_qb), (w4_q, z_qb)), [nc.scalar.copy, nc.vector.tensor_copy] * 2)

@@ -89,11 +89,8 @@ def tile_picked_rvqres_none_p_kernel(
         book_t = load_list(book, "book_t")
         offs_t = load_list(offs, "offs_t")
         c2_t = load_list(c2, "c2_t")
-        for q in range(4):
-            nc.sync.dma_start(
-                x_bytes[32 * q : 32 * q + 4, :].bitcast(I32),
-                x_scales[0, 4 * q : 4 * q + 4, :].bitcast(I32),
-            )
+        for r in range(4):
+            nc.sync.dma_start(x_bytes[r:P:32, :].bitcast(I32), x_scales[0, r:16:4, :].bitcast(I32))
         x_table = keep.tile([P, T], I32, name="x_table", align_bytes=64)
         nc.sync.dma_start(x_table[:], x_words[0].rearrange("p n t -> p (n t)").bitcast(I32))
         w2_raw = load_weight(w2, "w2_raw")

@@ -18,7 +18,6 @@ MULT = mybir.AluOpType.mult
 P = 128
 PACK = 4
 HALF = 256
-CHUNKS = (slice(0, 256), slice(256, 512))
 SHARE = 80
 
 
@@ -165,15 +164,13 @@ def tile_picked_rvqres_none_p_kernel(
         def woven_tile(name, count, tag=None):
             return keep.tile([P, PACK * count], BF16, name=name, tag=tag or name, align_bytes=64)
 
-        def weave_first(a):
-            cols = CHUNKS[a]
-            r1_g = woven_tile("r1_g%d" % a, cols.stop - cols.start)
+        def weave_first(cols, name):
+            r1_g = woven_tile(name, cols.stop - cols.start)
             nc.scalar.copy(*woven_views(r1_g[:], r1[:, :, cols], 4))
             return r1_g
 
-        def second_remainder(a, tag):
-            cols = CHUNKS[a]
-            z_g = woven_tile("z_g%d" % a, cols.stop - cols.start, tag)
+        def second_remainder(cols, name, tag):
+            z_g = woven_tile(name, cols.stop - cols.start, tag)
             dst, src = woven_views(z_g[:], r1[:, :, cols], 2)
             nc.vector.tensor_tensor(dst, src, woven_views(z_g[:], second[:, :, cols], 2)[1], ADD)
             return z_g
@@ -183,30 +180,33 @@ def tile_picked_rvqres_none_p_kernel(
             nc.scalar.copy(*woven_views(grouped[:], raw[:], 4))
             return grouped
 
-        def finish(a, banks, factors, engines):
-            count = CHUNKS[a].stop - CHUNKS[a].start
-            accs = [bank(b) for b in banks]
-            view = out[:, CHUNKS[a]].rearrange("(m p) j -> p m j", p=P)
-            for opens, (left, right) in zip((True, False), factors):
-                for m in range(PACK):
-                    product(accs[m][:, :count], left, rows(m), right, slice(0, count), opens, not opens)
+        def passes(accs, left, right, at, start, stop):
+            count = right[1].shape[1]
             for m in range(PACK):
-                staged = keep.tile([P, count], F32, name="staged%d_%d" % (a, m))
-                engines[m](staged[:], accs[m][:, :count])
+                product(accs[m][:, at : at + count], left, rows(m), right, slice(0, count), start, stop)
+
+        def store(h, accs, engines):
+            view = out[:, halves[h]].rearrange("(m p) j -> p m j", p=P)
+            for m in range(PACK):
+                staged = keep.tile([P, HALF], F32, name="staged%d_%d" % (h, m))
+                engines[m](staged[:], accs[m][:, :HALF])
                 nc.sync.dma_start(view[:, m, :], staged[:])
 
         for t in range(PACK):
             first_remainder(t, whole)
         w3_q = quantize(round_weight(w3_raw, "w3_g", "w1_1_codes")[:], "w3")
-        for m in range(2):
+        for m in range(3):
             product(bank(PACK + m)[:], w3_q, rows(m), x_book, whole, True, True)
-        z_ga = second_remainder(0, "w3_raw")
+        z_ga = second_remainder(halves[0], "z_ga", "w3_raw")
         w4_q = quantize(round_weight(w4_raw, "w4_g", "w2_g0")[:], "w4")
-        r1_g = [weave_first(a) for a in range(2)]
-        z_qa = quantize(z_ga[:], "z_0")
-        r1_qa = quantize(r1_g[0][:], "r1_0")
-        finish(0, (0, 1, 2, 3), ((w4_q, z_qa), (w3_q, r1_qa)), [nc.scalar.copy] * PACK)
-        z_gb = second_remainder(1, "r1_g0")
-        r1_qb = quantize(r1_g[1][:], "r1_1")
-        z_qb = quantize(z_gb[:], "z_1")
-        finish(1, (4, 5, 6, 7), ((w3_q, r1_qb), (w4_q, z_qb)), [nc.scalar.copy, nc.vector.tensor_copy] * 2)
+        r1_g = [weave_first(halves[h], "r1_g%d" % h) for h in range(2)]
+        accs = [[bank(PACK * h + m) for m in range(PACK)] for h in range(2)]
+        passes(accs[0], w4_q, quantize(z_ga[:], "z_a"), 0, True, False)
+        passes(accs[0], w3_q, quantize(r1_g[0][:], "r1_0"), 0, False, True)
+        store(0, accs[0], [nc.scalar.copy] * PACK)
+        passes(accs[1], w3_q, quantize(r1_g[1][:], "r1_1"), 0, True, False)
+        quarters = [slice(HALF + P * i, HALF + P * (i + 1)) for i in range(2)]
+        z_gb = [second_remainder(quarters[i], "z_gb%d" % i, ("r1_g0", "r1_g1")[i]) for i in range(2)]
+        for i in range(2):
+            passes(accs[1], w4_q, quantize(z_gb[i][:], "z_b%d" % i), P * i, False, i == 1)
+        store(1, accs[1], [nc.scalar.copy, nc.vector.tensor_copy] * 2)

@@ -19,6 +19,7 @@ P = 128
 PACK = 4
 HALF = 256
 SHARE = 80
+LEAD = 512
 
 
 def tile_picked_rvqres_none_p_kernel(
@@ -85,14 +86,16 @@ def tile_picked_rvqres_none_p_kernel(
         halves = [slice(h * HALF, (h + 1) * HALF) for h in range(2)]
         x_bytes = keep.tile([P, T], U8, name="x_bytes", align_bytes=64)
         nc.vector.memset(x_bytes[:].bitcast(I32), 0)
+        x_table = keep.tile([P, T], I32, name="x_table", align_bytes=64)
+        x_rows = x_words[0].rearrange("p n t -> p (n t)").bitcast(I32)
+        nc.sync.dma_start(x_table[:, :LEAD], x_rows[:, :LEAD])
         book_t = load_list(book, "book_t")
         offs_t = load_list(offs, "offs_t")
-        c2_t = load_list(c2, "c2_t")
         for r in range(4):
             nc.sync.dma_start(x_bytes[r:P:32, :].bitcast(I32), x_scales[0, r:16:4, :].bitcast(I32))
-        x_table = keep.tile([P, T], I32, name="x_table", align_bytes=64)
-        nc.sync.dma_start(x_table[:], x_words[0].rearrange("p n t -> p (n t)").bitcast(I32))
+        nc.sync.dma_start(x_table[:, LEAD:], x_rows[:, LEAD:])
         w2_raw = load_weight(w2, "w2_raw")
+        c2_t = load_list(c2, "c2_t")
         w1_raw = load_weight(w1, "w1_raw")
         c1_t = load_list(c1, "c1_t")
         w3_raw = load_weight(w3, "w3_raw")
@@ -106,8 +109,6 @@ def tile_picked_rvqres_none_p_kernel(
         nc.vector.tensor_copy(x_book[1][:], x_bytes[:].indirect(book_t[:]))
         nc.vector.tensor_copy(pick_scales[:], x_bytes[:].indirect(offs_t[:]))
         nc.vector.tensor_copy(x_book[0][:], x_table[:].bitcast(U32).indirect(book_t[:]))
-        early_words = keep.tile([P, HALF], U32, name="early_words", align_bytes=64)
-        nc.vector.tensor_copy(early_words[:], x_table[:].bitcast(U32).indirect(entries(offs_t, 0, HALF)))
 
         w2_g = [pair_tile("w2_g%d" % u, "w2_g%d" % u) for u in range(2)]
         dst, src = dealt_views(w2_g[0][:], w2_raw, 0)
@@ -119,9 +120,9 @@ def tile_picked_rvqres_none_p_kernel(
             nc.vector.quantize_mx(
                 out=w2_q[0][0][:, rows(t)].bitcast(FP8X4), scales=w2_q[0][1][:, rows(t)], in_=w2_g[0][:, H * t : H * (t + 1)]
             )
-        late_words = keep.tile([P, HALF], U32, name="late_words", tag="w2_g0", align_bytes=64)
-        nc.vector.tensor_copy(late_words[:], x_table[:].bitcast(U32).indirect(entries(offs_t, HALF, HALF)))
-        x_pick = [(early_words, pick_scales[:, halves[0]]), (late_words, pick_scales[:, halves[1]])]
+        pick_words = keep.tile([P, S], U32, name="pick_words", tag="w2_g0", align_bytes=64)
+        nc.vector.tensor_copy(pick_words[:], x_table[:].bitcast(U32).indirect(offs_t[:]))
+        x_pick = [(pick_words[:, halves[h]], pick_scales[:, halves[h]]) for h in range(2)]
         w2_q.append(quantize(w2_g[1][:], "w2_1"))
 
         whole = slice(0, 512)

@@ -172,8 +172,8 @@ def tile_picked_rvqres_none_p_kernel(
 
         def second_remainder(cols, name, tag):
             z_g = woven_tile(name, cols.stop - cols.start, tag)
-            dst, src = woven_views(z_g[:], r1[:, :, cols], 2)
-            nc.vector.tensor_tensor(dst, src, woven_views(z_g[:], second[:, :, cols], 2)[1], ADD)
+            dst, src = woven_views(z_g[:], r1[:, :, cols], 4)
+            nc.vector.tensor_tensor(dst, src, woven_views(z_g[:], second[:, :, cols], 4)[1], ADD)
             return z_g
 
         def round_weight(raw, name, tag):

@@ -122,15 +122,15 @@ def tile_picked_rvqres_none_p_kernel(
             )
         pick_words = keep.tile([P, S], U32, name="pick_words", tag="w2_g0", align_bytes=64)
         nc.vector.tensor_copy(pick_words[:], x_table[:].bitcast(U32).indirect(offs_t[:]))
-        x_pick = [(pick_words[:, halves[h]], pick_scales[:, halves[h]]) for h in range(2)]
+        x_pick = (pick_words, pick_scales)
         w2_q.append(quantize(w2_g[1][:], "w2_1"))
 
         whole = slice(0, 512)
         neg_c = [keep.tile([P, 2 * V], F32, name="neg_c%d" % t) for t in range(PACK)]
-        first_acc = [bank(PACK + h) for h in range(2)]
-        for h in range(2):
-            product(first_acc[h][:, :HALF], w2_q[0], rows(0), x_book, halves[h], True, True)
-            nc.scalar.mul(neg_c[0][:, halves[h]], first_acc[h][:, :HALF], -1.0)
+        for i in range(PACK):
+            first_acc = bank(PACK + i)
+            product(first_acc[:, :P], w2_q[0], rows(0), x_book, rows(i), True, True)
+            nc.scalar.mul(neg_c[0][:, rows(i)], first_acc[:, :P], -1.0)
         c_acc = [None] + [bank(t) for t in range(1, PACK)]
         for t in range(1, PACK):
             product(c_acc[t][:], w2_q[t // 2], rows(t % 2), x_book, whole, True, True)
@@ -152,8 +152,7 @@ def tile_picked_rvqres_none_p_kernel(
 
         y_acc = [bank(PACK + t) for t in range(PACK)]
         for t in range(PACK):
-            for h in range(2):
-                product(y_acc[t][:, halves[h]], w1_q[t // 2], rows(t % 2), x_pick[h], halves[0], True, True)
+            product(y_acc[t][:], w1_q[t // 2], rows(t % 2), x_pick, whole, True, True)
         y = keep.tile([P, PACK, S], F32, name="y")
         r1 = keep.tile([P, PACK, S], F32, name="r1")
 

@@ -110,6 +110,9 @@ def tile_picked_rvqres_none_p_kernel(
         nc.vector.tensor_copy(pick_scales[:], x_bytes[:].indirect(offs_t[:]))
         nc.vector.tensor_copy(x_book[0][:], x_table[:].bitcast(U32).indirect(book_t[:]))
 
+        early_words = keep.tile([P, HALF], U32, name="early_words", align_bytes=64)
+        nc.vector.tensor_copy(early_words[:], x_table[:].bitcast(U32).indirect(entries(offs_t, 0, HALF)))
+
         w2_g = [pair_tile("w2_g%d" % u, "w2_g%d" % u) for u in range(2)]
         dst, src = dealt_views(w2_g[0][:], w2_raw, 0)
         nc.vector.tensor_copy(dst[:, :SHARE], src[:, :SHARE])
@@ -120,9 +123,8 @@ def tile_picked_rvqres_none_p_kernel(
             nc.vector.quantize_mx(
                 out=w2_q[0][0][:, rows(t)].bitcast(FP8X4), scales=w2_q[0][1][:, rows(t)], in_=w2_g[0][:, H * t : H * (t + 1)]
             )
-        pick_words = keep.tile([P, S], U32, name="pick_words", tag="w2_g0", align_bytes=64)
-        nc.vector.tensor_copy(pick_words[:], x_table[:].bitcast(U32).indirect(offs_t[:]))
-        x_pick = (pick_words, pick_scales)
+        late_words = keep.tile([P, HALF], U32, name="late_words", tag="w2_g0", align_bytes=64)
+        nc.vector.tensor_copy(late_words[:], x_table[:].bitcast(U32).indirect(entries(offs_t, HALF, HALF)))
         w2_q.append(quantize(w2_g[1][:], "w2_1"))
 
         whole = slice(0, 512)
@@ -130,7 +132,10 @@ def tile_picked_rvqres_none_p_kernel(
         for i in range(PACK):
             first_acc = bank(PACK + i)
             product(first_acc[:, :P], w2_q[0], rows(0), x_book, rows(i), True, True)
-            nc.scalar.mul(neg_c[0][:, rows(i)], first_acc[:, :P], -1.0)
+            if i < PACK - 1:
+                nc.scalar.mul(neg_c[0][:, rows(i)], first_acc[:, :P], -1.0)
+            else:
+                nc.vector.tensor_scalar_mul(neg_c[0][:, rows(i)], first_acc[:, :P], -1.0)
         c_acc = [None] + [bank(t) for t in range(1, PACK)]
         for t in range(1, PACK):
             product(c_acc[t][:], w2_q[t // 2], rows(t % 2), x_book, whole, True, True)
@@ -152,7 +157,8 @@ def tile_picked_rvqres_none_p_kernel(
 
         y_acc = [bank(PACK + t) for t in range(PACK)]
         for t in range(PACK):
-            product(y_acc[t][:], w1_q[t // 2], rows(t % 2), x_pick, whole, True, True)
+            for words, cols in zip((early_words, late_words), halves):
+                product(y_acc[t][:, cols], w1_q[t // 2], rows(t % 2), (words, pick_scales[:, cols]), halves[0], True, True)
         y = keep.tile([P, PACK, S], F32, name="y")
         r1 = keep.tile([P, PACK, S], F32, name="r1")
 

@@ -18,8 +18,8 @@ MULT = mybir.AluOpType.mult
 P = 128
 PACK = 4
 HALF = 256
-SHARE = 80
-LEAD = 512
+SHARE = 64
+LEAD = 384
 
 
 def tile_picked_rvqres_none_p_kernel(

@@ -14,6 +14,7 @@ U8 = mybir.dt.uint8
 FP8X4 = mybir.dt.float8_e4m3fn_x4
 ADD = mybir.AluOpType.add
 MULT = mybir.AluOpType.mult
+COPY = mybir.ActivationFunctionType.Copy
 
 P = 128
 PACK = 4
@@ -31,20 +32,21 @@ def tile_picked_rvqres_none_p_kernel(
         keep = ctx.enter_context(tc.tile_pool(name="keep", bufs=1))
         psum = ctx.enter_context(tc.psum_pool(name="psum", bufs=1))
 
+        def tile(name, shape, dtype, tag=None):
+            return keep.tile(shape, dtype, name=name, tag=tag or name, align_bytes=64)
+
         def load_list(src, name):
-            tile = lists.tile([P, S // 16], U16, name=name)
-            nc.sync.dma_start(tile[:], src)
-            return tile
+            offsets = lists.tile([P, S // 16], U16, name=name)
+            nc.sync.dma_start(offsets[:], src)
+            return offsets
 
         def load_weight(w, name):
-            raw = keep.tile([P, PACK, w.shape[1]], F32, name=name, tag=name, align_bytes=64)
+            raw = tile(name, [P, PACK, w.shape[1]], F32)
             nc.sync.dma_start(raw[:], w.rearrange("(p j) n -> p j n", j=PACK))
             return raw
 
         def operand(name, width, tag=None):
-            codes = keep.tile([P, width], U32, name=name + "_codes", tag=tag or name + "_codes", align_bytes=64)
-            scales = keep.tile([P, width], U8, name=name + "_scales", tag=name + "_scales", align_bytes=64)
-            return codes, scales
+            return tile(name + "_codes", [P, width], U32, tag), tile(name + "_scales", [P, width], U8)
 
         def quantize(grouped, name, tag=None):
             codes, scales = operand(name, grouped.shape[1] // PACK, tag)
@@ -68,10 +70,10 @@ def tile_picked_rvqres_none_p_kernel(
                 raw[:].rearrange("p j (m t) -> p m j t", t=PACK)[:, :, :, 2 * u : 2 * u + 2],
             )
 
-        def woven_views(grouped, planes, run):
+        def woven_views(grouped, planes):
             return (
-                grouped.rearrange("p (c i t) -> p c t i", t=PACK, i=run),
-                planes.rearrange("p t (c i) -> p c t i", i=run),
+                grouped.rearrange("p (c i t) -> p c t i", t=PACK, i=4),
+                planes.rearrange("p t (c i) -> p c t i", i=4),
             )
 
         def bank(b):
@@ -80,13 +82,14 @@ def tile_picked_rvqres_none_p_kernel(
         def rows(t):
             return slice(P * t, P * (t + 1))
 
-        def entries(tile, first, count):
-            return tile[:, first // 16 : (first + count) // 16]
+        def entries(offsets, cols):
+            return offsets[:, cols.start // 16 : cols.stop // 16]
 
         halves = [slice(h * HALF, (h + 1) * HALF) for h in range(2)]
-        x_bytes = keep.tile([P, T], U8, name="x_bytes", align_bytes=64)
+        whole = slice(0, 512)
+        x_bytes = tile("x_bytes", [P, T], U8)
         nc.vector.memset(x_bytes[:].bitcast(I32), 0)
-        x_table = keep.tile([P, T], I32, name="x_table", align_bytes=64)
+        x_table = tile("x_table", [P, T], I32)
         x_rows = x_words[0].rearrange("p n t -> p (n t)").bitcast(I32)
         nc.sync.dma_start(x_table[:, :LEAD], x_rows[:, :LEAD])
         book_t = load_list(book, "book_t")
@@ -95,25 +98,21 @@ def tile_picked_rvqres_none_p_kernel(
             nc.sync.dma_start(x_bytes[r:P:32, :].bitcast(I32), x_scales[0, r:16:4, :].bitcast(I32))
         nc.sync.dma_start(x_table[:, LEAD:], x_rows[:, LEAD:])
         w2_raw = load_weight(w2, "w2_raw")
-        c2_t = load_list(c2, "c2_t")
-        w1_raw = load_weight(w1, "w1_raw")
         c1_t = load_list(c1, "c1_t")
+        w1_raw = load_weight(w1, "w1_raw")
+        c2_t = load_list(c2, "c2_t")
         w3_raw = load_weight(w3, "w3_raw")
         w4_raw = load_weight(w4, "w4_raw")
 
-        def pair_tile(name, tag):
-            return keep.tile([P, 2 * H], BF16, name=name, tag=tag, align_bytes=64)
-
         x_book = operand("x_book", V)
-        pick_scales = keep.tile([P, S], U8, name="pick_scales", align_bytes=64)
+        pick_scales = tile("pick_scales", [P, S], U8)
         nc.vector.tensor_copy(x_book[1][:], x_bytes[:].indirect(book_t[:]))
         nc.vector.tensor_copy(pick_scales[:], x_bytes[:].indirect(offs_t[:]))
         nc.vector.tensor_copy(x_book[0][:], x_table[:].bitcast(U32).indirect(book_t[:]))
+        early_words = tile("early_words", [P, HALF], U32)
+        nc.vector.tensor_copy(early_words[:], x_table[:].bitcast(U32).indirect(entries(offs_t, halves[0])))
 
-        early_words = keep.tile([P, HALF], U32, name="early_words", align_bytes=64)
-        nc.vector.tensor_copy(early_words[:], x_table[:].bitcast(U32).indirect(entries(offs_t, 0, HALF)))
-
-        w2_g = [pair_tile("w2_g%d" % u, "w2_g%d" % u) for u in range(2)]
+        w2_g = [tile("w2_g%d" % u, [P, 2 * H], BF16) for u in range(2)]
         dst, src = dealt_views(w2_g[0][:], w2_raw, 0)
         nc.vector.tensor_copy(dst[:, :SHARE], src[:, :SHARE])
         nc.scalar.copy(dst[:, SHARE:], src[:, SHARE:])
@@ -123,68 +122,68 @@ def tile_picked_rvqres_none_p_kernel(
             nc.vector.quantize_mx(
                 out=w2_q[0][0][:, rows(t)].bitcast(FP8X4), scales=w2_q[0][1][:, rows(t)], in_=w2_g[0][:, H * t : H * (t + 1)]
             )
-        late_words = keep.tile([P, HALF], U32, name="late_words", tag="w2_g0", align_bytes=64)
-        nc.vector.tensor_copy(late_words[:], x_table[:].bitcast(U32).indirect(entries(offs_t, HALF, HALF)))
+        late_words = tile("late_words", [P, HALF], U32, "w2_g0")
+        nc.vector.tensor_copy(late_words[:], x_table[:].bitcast(U32).indirect(entries(offs_t, halves[1])))
         w2_q.append(quantize(w2_g[1][:], "w2_1"))
 
-        whole = slice(0, 512)
-        neg_c = [keep.tile([P, 2 * V], F32, name="neg_c%d" % t) for t in range(PACK)]
+        half_c = [tile("half_c%d" % t, [P, V], F32) for t in range(PACK)]
         for i in range(PACK):
             first_acc = bank(PACK + i)
             product(first_acc[:, :P], w2_q[0], rows(0), x_book, rows(i), True, True)
-            if i < PACK - 1:
-                nc.scalar.mul(neg_c[0][:, rows(i)], first_acc[:, :P], -1.0)
-            else:
-                nc.vector.tensor_scalar_mul(neg_c[0][:, rows(i)], first_acc[:, :P], -1.0)
+            nc.scalar.mul(half_c[0][:, rows(i)], first_acc[:, :P], -0.5)
         c_acc = [None] + [bank(t) for t in range(1, PACK)]
         for t in range(1, PACK):
             product(c_acc[t][:], w2_q[t // 2], rows(t % 2), x_book, whole, True, True)
-        second = keep.tile([P, PACK, S], F32, name="second")
 
-        def look_up_second(t):
-            if t:
-                nc.scalar.mul(neg_c[t][:, :V], c_acc[t][:], -1.0)
-            nc.vector.tensor_scalar(second[:, t, :], neg_c[t][:].indirect(c2_t[:]), 0.5, 0.0, MULT, ADD)
+        def look_up(offsets, cols, name):
+            found = tile(name, [P, PACK, cols.stop - cols.start], F32)
+            for t in range(PACK):
+                nc.scalar.activation(found[:, t, :], half_c[t][:].indirect(entries(offsets, cols)), COPY)
+            return found
 
-        w1_g = [pair_tile("w1_g%d" % u, "w2_%d_codes" % u) for u in range(2)]
-        w1_q = []
-        look_up_second(0)
-        for u in range(2):
-            look_up_second(1 + u)
-            nc.scalar.copy(*dealt_views(w1_g[u][:], w1_raw, u))
-            w1_q.append(quantize(w1_g[u][:], "w1_%d" % u))
-        look_up_second(3)
-
-        y_acc = [bank(PACK + t) for t in range(PACK)]
+        first = [tile("first0", [P, PACK, HALF], F32)]
         for t in range(PACK):
-            for words, cols in zip((early_words, late_words), halves):
-                product(y_acc[t][:, cols], w1_q[t // 2], rows(t % 2), (words, pick_scales[:, cols]), halves[0], True, True)
-        y = keep.tile([P, PACK, S], F32, name="y")
-        r1 = keep.tile([P, PACK, S], F32, name="r1")
+            if t:
+                nc.scalar.mul(half_c[t][:], c_acc[t][:], -0.5)
+            nc.scalar.activation(first[0][:, t, :], half_c[t][:].indirect(entries(c1_t, halves[0])), COPY)
+        second_a = look_up(c2_t, halves[0], "second_a")
+        first.append(look_up(c1_t, halves[1], "first1"))
+        quarters = [slice(HALF + P * i, HALF + P * (i + 1)) for i in range(2)]
+        second_b = [look_up(c2_t, quarters[i], "second_b%d" % i) for i in range(2)]
 
-        def first_remainder(t, cols):
-            nc.scalar.copy(y[:, t, cols], y_acc[t][:, cols])
-            offsets = entries(c1_t, cols.start, cols.stop - cols.start)
-            nc.vector.tensor_tensor(r1[:, t, cols], neg_c[t][:].indirect(offsets), y[:, t, cols], ADD)
+        w1_g = [tile("w1_g%d" % u, [P, 2 * H], BF16) for u in range(2)]
+        for u in range(2):
+            nc.vector.tensor_copy(*dealt_views(w1_g[u][:], w1_raw, u))
+        w1_q = [quantize(w1_g[u][:], "w1_%d" % u) for u in range(2)]
 
-        def woven_tile(name, count, tag=None):
-            return keep.tile([P, PACK * count], BF16, name=name, tag=tag or name, align_bytes=64)
+        y_acc = [[bank(PACK + 2 * h + u) for u in range(2)] for h in range(2)]
+        for h, words in enumerate((early_words, late_words)):
+            for t in range(PACK):
+                acc = y_acc[h][t // 2][:, halves[t % 2]]
+                product(acc, w1_q[t // 2], rows(t % 2), (words, pick_scales[:, halves[h]]), halves[0], True, True)
+        r1 = [tile("r1_%d" % h, [P, PACK, HALF], F32) for h in range(2)]
 
-        def weave_first(cols, name):
-            r1_g = woven_tile(name, cols.stop - cols.start)
-            nc.scalar.copy(*woven_views(r1_g[:], r1[:, :, cols], 4))
-            return r1_g
+        def first_remainder(h, u):
+            pair = slice(2 * u, 2 * u + 2)
+            nc.vector.scalar_tensor_tensor(
+                r1[h][:, pair, :].rearrange("p t c -> p (t c)"),
+                first[h][:, pair, :].rearrange("p t c -> p (t c)"),
+                2.0,
+                y_acc[h][u][:],
+                MULT,
+                ADD,
+            )
 
-        def second_remainder(cols, name, tag):
-            z_g = woven_tile(name, cols.stop - cols.start, tag)
-            dst, src = woven_views(z_g[:], r1[:, :, cols], 4)
-            nc.vector.tensor_tensor(dst, src, woven_views(z_g[:], second[:, :, cols], 4)[1], ADD)
-            return z_g
-
-        def round_weight(raw, name, tag):
-            grouped = woven_tile(name, N, tag)
-            nc.scalar.copy(*woven_views(grouped[:], raw[:], 4))
+        def weave(planes, name):
+            grouped = tile(name, [P, PACK * planes.shape[2]], BF16)
+            nc.vector.tensor_copy(*woven_views(grouped[:], planes))
             return grouped
+
+        def second_remainder(planes, found, name):
+            z_g = tile(name, [P, PACK * planes.shape[2]], BF16)
+            dst, src = woven_views(z_g[:], planes)
+            nc.vector.tensor_tensor(dst, src, woven_views(z_g[:], found[:])[1], ADD)
+            return z_g
 
         def passes(accs, left, right, at, start, stop):
             count = right[1].shape[1]
@@ -194,25 +193,28 @@ def tile_picked_rvqres_none_p_kernel(
         def store(h, accs, engines):
             view = out[:, halves[h]].rearrange("(m p) j -> p m j", p=P)
             for m in range(PACK):
-                staged = keep.tile([P, HALF], F32, name="staged%d_%d" % (h, m))
+                staged = tile("staged%d_%d" % (h, m), [P, HALF], F32)
                 engines[m](staged[:], accs[m][:, :HALF])
                 nc.sync.dma_start(view[:, m, :], staged[:])
 
-        for t in range(PACK):
-            first_remainder(t, whole)
-        w3_q = quantize(round_weight(w3_raw, "w3_g", "w1_1_codes")[:], "w3")
-        for m in range(3):
-            product(bank(PACK + m)[:], w3_q, rows(m), x_book, whole, True, True)
-        z_ga = second_remainder(halves[0], "z_ga", "w3_raw")
-        w4_q = quantize(round_weight(w4_raw, "w4_g", "w2_g0")[:], "w4")
-        r1_g = [weave_first(halves[h], "r1_g%d" % h) for h in range(2)]
+        w3_g = weave(w3_raw[:], "w3_g")
+        first_remainder(0, 0)
+        first_remainder(0, 1)
+        w3_q = quantize(w3_g[:], "w3")
+        r1_ga = weave(r1[0][:], "r1_ga")
+        w4_g = weave(w4_raw[:], "w4_g")
         accs = [[bank(PACK * h + m) for m in range(PACK)] for h in range(2)]
-        passes(accs[0], w4_q, quantize(z_ga[:], "z_a"), 0, True, False)
-        passes(accs[0], w3_q, quantize(r1_g[0][:], "r1_0"), 0, False, True)
+        passes(accs[0], w3_q, quantize(r1_ga[:], "r1_a"), 0, True, False)
+        z_ga = second_remainder(r1[0][:], second_a, "z_ga")
+        w4_q = quantize(w4_g[:], "w4")
+        passes(accs[0], w4_q, quantize(z_ga[:], "z_a"), 0, False, True)
+        first_remainder(1, 0)
+        first_remainder(1, 1)
         store(0, accs[0], [nc.scalar.copy] * PACK)
-        passes(accs[1], w3_q, quantize(r1_g[1][:], "r1_1"), 0, True, False)
-        quarters = [slice(HALF + P * i, HALF + P * (i + 1)) for i in range(2)]
-        z_gb = [second_remainder(quarters[i], "z_gb%d" % i, ("r1_g0", "r1_g1")[i]) for i in range(2)]
+        r1_gb = weave(r1[1][:], "r1_gb")
+        z_gb = [second_remainder(r1[1][:, :, rows(0)], second_b[0], "z_gb0")]
+        passes(accs[1], w3_q, quantize(r1_gb[:], "r1_b"), 0, True, False)
+        z_gb.append(second_remainder(r1[1][:, :, rows(1)], second_b[1], "z_gb1"))
         for i in range(2):
             passes(accs[1], w4_q, quantize(z_gb[i][:], "z_b%d" % i), P * i, False, i == 1)
         store(1, accs[1], [nc.scalar.copy, nc.vector.tensor_copy] * 2)

@@ -19,7 +19,7 @@ COPY = mybir.ActivationFunctionType.Copy
 P = 128
 PACK = 4
 HALF = 256
-SHARE = 64
+SHARE = 80
 LEAD = 384
 
 
@@ -109,24 +109,22 @@ def tile_picked_rvqres_none_p_kernel(
         nc.vector.tensor_copy(x_book[1][:], x_bytes[:].indirect(book_t[:]))
         nc.vector.tensor_copy(pick_scales[:], x_bytes[:].indirect(offs_t[:]))
         nc.vector.tensor_copy(x_book[0][:], x_table[:].bitcast(U32).indirect(book_t[:]))
-        early_words = tile("early_words", [P, HALF], U32)
-        nc.vector.tensor_copy(early_words[:], x_table[:].bitcast(U32).indirect(entries(offs_t, halves[0])))
 
         w2_g = [tile("w2_g%d" % u, [P, 2 * H], BF16) for u in range(2)]
-        dst, src = dealt_views(w2_g[0][:], w2_raw, 0)
-        nc.vector.tensor_copy(dst[:, :SHARE], src[:, :SHARE])
-        nc.scalar.copy(dst[:, SHARE:], src[:, SHARE:])
-        nc.scalar.copy(*dealt_views(w2_g[1][:], w2_raw, 1))
+        for u, share in enumerate((SHARE, P - SHARE)):
+            dst, src = dealt_views(w2_g[u][:], w2_raw, u)
+            nc.vector.tensor_copy(dst[:, :share], src[:, :share])
+            nc.scalar.copy(dst[:, share:], src[:, share:])
         w2_q = [operand("w2_0", HALF)]
         for t in range(2):
             nc.vector.quantize_mx(
                 out=w2_q[0][0][:, rows(t)].bitcast(FP8X4), scales=w2_q[0][1][:, rows(t)], in_=w2_g[0][:, H * t : H * (t + 1)]
             )
-        late_words = tile("late_words", [P, HALF], U32, "w2_g0")
-        nc.vector.tensor_copy(late_words[:], x_table[:].bitcast(U32).indirect(entries(offs_t, halves[1])))
+        pick_words = tile("pick_words", [P, S], U32, "w2_g0")
+        nc.vector.tensor_copy(pick_words[:], x_table[:].bitcast(U32).indirect(offs_t[:]))
         w2_q.append(quantize(w2_g[1][:], "w2_1"))
 
-        half_c = [tile("half_c%d" % t, [P, V], F32) for t in range(PACK)]
+        half_c = [tile("half_c%d" % t, [P, 2 * V], F32) for t in range(PACK)]
         for i in range(PACK):
             first_acc = bank(PACK + i)
             product(first_acc[:, :P], w2_q[0], rows(0), x_book, rows(i), True, True)
@@ -135,44 +133,16 @@ def tile_picked_rvqres_none_p_kernel(
         for t in range(1, PACK):
             product(c_acc[t][:], w2_q[t // 2], rows(t % 2), x_book, whole, True, True)
 
-        def look_up(offsets, cols, name):
-            found = tile(name, [P, PACK, cols.stop - cols.start], F32)
-            for t in range(PACK):
-                nc.scalar.activation(found[:, t, :], half_c[t][:].indirect(entries(offsets, cols)), COPY)
-            return found
-
-        first = [tile("first0", [P, PACK, HALF], F32)]
+        first = tile("first", [P, PACK, S], F32)
         for t in range(PACK):
             if t:
-                nc.scalar.mul(half_c[t][:], c_acc[t][:], -0.5)
-            nc.scalar.activation(first[0][:, t, :], half_c[t][:].indirect(entries(c1_t, halves[0])), COPY)
-        second_a = look_up(c2_t, halves[0], "second_a")
-        first.append(look_up(c1_t, halves[1], "first1"))
-        quarters = [slice(HALF + P * i, HALF + P * (i + 1)) for i in range(2)]
-        second_b = [look_up(c2_t, quarters[i], "second_b%d" % i) for i in range(2)]
-
-        w1_g = [tile("w1_g%d" % u, [P, 2 * H], BF16) for u in range(2)]
-        for u in range(2):
-            nc.vector.tensor_copy(*dealt_views(w1_g[u][:], w1_raw, u))
-        w1_q = [quantize(w1_g[u][:], "w1_%d" % u) for u in range(2)]
-
-        y_acc = [[bank(PACK + 2 * h + u) for u in range(2)] for h in range(2)]
-        for h, words in enumerate((early_words, late_words)):
+                nc.scalar.mul(half_c[t][:, :V], c_acc[t][:], -0.5)
+            nc.scalar.activation(first[:, t, :], half_c[t][:].indirect(c1_t[:]), COPY)
+        second = []
+        for h, tag in enumerate(("w2_1_codes", "x_book_codes")):
+            second.append(tile("second%d" % h, [P, PACK, HALF], F32, tag))
             for t in range(PACK):
-                acc = y_acc[h][t // 2][:, halves[t % 2]]
-                product(acc, w1_q[t // 2], rows(t % 2), (words, pick_scales[:, halves[h]]), halves[0], True, True)
-        r1 = [tile("r1_%d" % h, [P, PACK, HALF], F32) for h in range(2)]
-
-        def first_remainder(h, u):
-            pair = slice(2 * u, 2 * u + 2)
-            nc.vector.scalar_tensor_tensor(
-                r1[h][:, pair, :].rearrange("p t c -> p (t c)"),
-                first[h][:, pair, :].rearrange("p t c -> p (t c)"),
-                2.0,
-                y_acc[h][u][:],
-                MULT,
-                ADD,
-            )
+                nc.scalar.activation(second[h][:, t, :], half_c[t][:].indirect(entries(c2_t, halves[h])), COPY)
 
         def weave(planes, name):
             grouped = tile(name, [P, PACK * planes.shape[2]], BF16)
@@ -182,39 +152,69 @@ def tile_picked_rvqres_none_p_kernel(
         def second_remainder(planes, found, name):
             z_g = tile(name, [P, PACK * planes.shape[2]], BF16)
             dst, src = woven_views(z_g[:], planes)
-            nc.vector.tensor_tensor(dst, src, woven_views(z_g[:], found[:])[1], ADD)
+            nc.vector.tensor_tensor(dst, src, woven_views(z_g[:], found)[1], ADD)
             return z_g
 
-        def passes(accs, left, right, at, start, stop):
-            count = right[1].shape[1]
-            for m in range(PACK):
-                product(accs[m][:, at : at + count], left, rows(m), right, slice(0, count), start, stop)
+        def picked_products(u, tag):
+            w1_q = quantize(w1_g[u][:], "w1_%d" % u, tag)
+            for e in range(2):
+                y_acc.append(bank(PACK + 2 * u + e))
+                product(y_acc[-1][:], w1_q, rows(e), (pick_words, pick_scales), whole, True, True)
 
-        def store(h, accs, engines):
-            view = out[:, halves[h]].rearrange("(m p) j -> p m j", p=P)
-            for m in range(PACK):
-                staged = tile("staged%d_%d" % (h, m), [P, HALF], F32)
-                engines[m](staged[:], accs[m][:, :HALF])
-                nc.sync.dma_start(view[:, m, :], staged[:])
+        def first_remainder(t):
+            nc.vector.scalar_tensor_tensor(r1[:, t, :], first[:, t, :], 2.0, y_acc[t][:], MULT, ADD)
 
-        w3_g = weave(w3_raw[:], "w3_g")
-        first_remainder(0, 0)
-        first_remainder(0, 1)
-        w3_q = quantize(w3_g[:], "w3")
-        r1_ga = weave(r1[0][:], "r1_ga")
+        def passes(acc, ms, left, right, cols, start, stop):
+            count = cols.stop - cols.start
+            for i, m in enumerate(ms):
+                product(
+                    acc[:, count * i : count * (i + 1)], left, rows(m), right, cols, start and i == 0, stop and i == len(ms) - 1
+                )
+
+        w1_g = [tile("w1_g%d" % u, [P, 2 * H], BF16) for u in range(2)]
+        for u in range(2):
+            nc.vector.tensor_copy(*dealt_views(w1_g[u][:], w1_raw, u))
+        y_acc = []
+        for u in range(2):
+            picked_products(u, None)
+        w3_g = [weave(w3_raw[:, :, halves[h]], "w3_g%d" % h) for h in range(2)]
+        w3_q = operand("w3", N)
+        for h in range(2):
+            nc.vector.quantize_mx(out=w3_q[0][:, halves[h]].bitcast(FP8X4), scales=w3_q[1][:, halves[h]], in_=w3_g[h][:])
         w4_g = weave(w4_raw[:], "w4_g")
-        accs = [[bank(PACK * h + m) for m in range(PACK)] for h in range(2)]
-        passes(accs[0], w3_q, quantize(r1_ga[:], "r1_a"), 0, True, False)
-        z_ga = second_remainder(r1[0][:], second_a, "z_ga")
-        w4_q = quantize(w4_g[:], "w4")
-        passes(accs[0], w4_q, quantize(z_ga[:], "z_a"), 0, False, True)
-        first_remainder(1, 0)
-        first_remainder(1, 1)
-        store(0, accs[0], [nc.scalar.copy] * PACK)
-        r1_gb = weave(r1[1][:], "r1_gb")
-        z_gb = [second_remainder(r1[1][:, :, rows(0)], second_b[0], "z_gb0")]
-        passes(accs[1], w3_q, quantize(r1_gb[:], "r1_b"), 0, True, False)
-        z_gb.append(second_remainder(r1[1][:, :, rows(1)], second_b[1], "z_gb1"))
+        r1 = tile("r1", [P, PACK, S], F32, "w4_raw")
+        for t in range(PACK):
+            first_remainder(t)
+
+        pairs = ((0, 1), (2, 3))
+        out_rows = out.rearrange("(m p) j -> p m j", p=P)
+        r1_ga = weave(r1[:, :, halves[0]], "r1_ga")
+        r1_gb = weave(r1[:, :, halves[1]], "r1_gb")
+        r1_qa = quantize(r1_ga[:], "r1_a")
+        r1_qb = quantize(r1_gb[:], "r1_b")
+        z_ga = second_remainder(r1[:, :, halves[0]], second[0][:], "z_ga")
+        w4_q = quantize(w4_g[:], "w4", "r1_gb")
+        z_qa = quantize(z_ga[:], "z_a")
+        acc_a = [bank(u) for u in range(2)]
+        for u in range(2):
+            passes(acc_a[u], pairs[u], w3_q, r1_qa, halves[0], True, False)
+        acc_b = [[bank(2 + 2 * i + u) for u in range(2)] for i in range(2)]
         for i in range(2):
-            passes(accs[1], w4_q, quantize(z_gb[i][:], "z_b%d" % i), P * i, False, i == 1)
-        store(1, accs[1], [nc.scalar.copy, nc.vector.tensor_copy] * 2)
+            for u in range(2):
+                passes(acc_b[i][u], pairs[u], w3_q, r1_qb, rows(i), True, False)
+        for u in range(2):
+            passes(acc_a[u], pairs[u], w4_q, z_qa, halves[0], False, True)
+            staged = tile("staged%d" % u, [P, 2, HALF], F32, "half_c%d" % (2 + u))
+            nc.scalar.copy(staged[:].rearrange("p m j -> p (m j)"), acc_a[u][:])
+            nc.sync.dma_start(out_rows[:, 2 * u : 2 * u + 2, halves[0]], staged[:])
+
+        quarters = [slice(HALF + P * i, HALF + P * (i + 1)) for i in range(2)]
+        z_gb = [second_remainder(r1[:, :, quarters[i]], second[1][:, :, rows(i)], "z_gb%d" % i) for i in range(2)]
+        staged_b = [tile("staged_b%d" % u, [P, 2, HALF], F32) for u in range(2)]
+        for i in range(2):
+            z_qb = quantize(z_gb[i][:], "z_b%d" % i)
+            for u, copy in enumerate((nc.scalar.copy, nc.vector.tensor_copy)):
+                passes(acc_b[i][u], pairs[u], w4_q, z_qb, rows(0), False, True)
+                copy(staged_b[u][:, :, rows(i)], acc_b[i][u][:, :HALF].rearrange("p (m j) -> p m j", m=2))
+        for u in range(2):
+            nc.sync.dma_start(out_rows[:, 2 * u : 2 * u + 2, halves[1]], staged_b[u][:])

@@ -110,6 +110,8 @@ def tile_picked_rvqres_none_p_kernel(
         nc.vector.tensor_copy(pick_scales[:], x_bytes[:].indirect(offs_t[:]))
         nc.vector.tensor_copy(x_book[0][:], x_table[:].bitcast(U32).indirect(book_t[:]))
 
+        early_words = tile("early_words", [P, P], U32)
+        nc.vector.tensor_copy(early_words[:], x_table[:].bitcast(U32).indirect(entries(offs_t, rows(0))))
         w2_g = [tile("w2_g%d" % u, [P, 2 * H], BF16) for u in range(2)]
         for u, share in enumerate((SHARE, P - SHARE)):
             dst, src = dealt_views(w2_g[u][:], w2_raw, u)
@@ -120,11 +122,11 @@ def tile_picked_rvqres_none_p_kernel(
             nc.vector.quantize_mx(
                 out=w2_q[0][0][:, rows(t)].bitcast(FP8X4), scales=w2_q[0][1][:, rows(t)], in_=w2_g[0][:, H * t : H * (t + 1)]
             )
-        pick_words = tile("pick_words", [P, S], U32, "w2_g0")
-        nc.vector.tensor_copy(pick_words[:], x_table[:].bitcast(U32).indirect(offs_t[:]))
+        late_words = tile("late_words", [P, S - P], U32, "w2_g0")
+        nc.vector.tensor_copy(late_words[:], x_table[:].bitcast(U32).indirect(entries(offs_t, slice(P, S))))
         w2_q.append(quantize(w2_g[1][:], "w2_1"))
 
-        half_c = [tile("half_c%d" % t, [P, 2 * V], F32) for t in range(PACK)]
+        half_c = [tile("half_c%d" % t, [P, V], F32) for t in range(PACK)]
         for i in range(PACK):
             first_acc = bank(PACK + i)
             product(first_acc[:, :P], w2_q[0], rows(0), x_book, rows(i), True, True)
@@ -136,13 +138,15 @@ def tile_picked_rvqres_none_p_kernel(
         first = tile("first", [P, PACK, S], F32)
         for t in range(PACK):
             if t:
-                nc.scalar.mul(half_c[t][:, :V], c_acc[t][:], -0.5)
-            nc.scalar.activation(first[:, t, :], half_c[t][:].indirect(c1_t[:]), COPY)
+                nc.scalar.mul(half_c[t][:], c_acc[t][:], -0.5)
+            for cols in halves if t else (halves[0], rows(2)):
+                nc.scalar.activation(first[:, t, cols], half_c[t][:].indirect(entries(c1_t, cols)), COPY)
+        quarters = [slice(HALF + P * i, HALF + P * (i + 1)) for i in range(2)]
         second = []
-        for h, tag in enumerate(("w2_1_codes", "x_book_codes")):
-            second.append(tile("second%d" % h, [P, PACK, HALF], F32, tag))
+        for cols, tag in zip([halves[0]] + quarters, ("w2_1_codes", "x_book_codes", "x_book_scales")):
+            second.append(tile("second%d" % cols.start, [P, PACK, cols.stop - cols.start], F32, tag))
             for t in range(PACK):
-                nc.scalar.activation(second[h][:, t, :], half_c[t][:].indirect(entries(c2_t, halves[h])), COPY)
+                nc.scalar.activation(second[-1][:, t, :], half_c[t][:].indirect(entries(c2_t, cols)), COPY)
 
         def weave(planes, name):
             grouped = tile(name, [P, PACK * planes.shape[2]], BF16)
@@ -159,7 +163,10 @@ def tile_picked_rvqres_none_p_kernel(
             w1_q = quantize(w1_g[u][:], "w1_%d" % u, tag)
             for e in range(2):
                 y_acc.append(bank(PACK + 2 * u + e))
-                product(y_acc[-1][:], w1_q, rows(e), (pick_words, pick_scales), whole, True, True)
+                product(y_acc[-1][:, :P], w1_q, rows(e), (early_words, pick_scales), rows(0), True, True)
+                late = (late_words, pick_scales[:, P:])
+                product(y_acc[-1][:, P:HALF], w1_q, rows(e), late, rows(0), True, True)
+                product(y_acc[-1][:, HALF:], w1_q, rows(e), late, slice(P, S - P), True, True)
 
         def first_remainder(t):
             nc.vector.scalar_tensor_tensor(r1[:, t, :], first[:, t, :], 2.0, y_acc[t][:], MULT, ADD)
@@ -177,44 +184,50 @@ def tile_picked_rvqres_none_p_kernel(
         y_acc = []
         for u in range(2):
             picked_products(u, None)
+        nc.vector.tensor_copy(first[:, 0, rows(3)], half_c[0][:].indirect(entries(c1_t, rows(3))))
         w3_g = [weave(w3_raw[:, :, halves[h]], "w3_g%d" % h) for h in range(2)]
         w3_q = operand("w3", N)
         for h in range(2):
             nc.vector.quantize_mx(out=w3_q[0][:, halves[h]].bitcast(FP8X4), scales=w3_q[1][:, halves[h]], in_=w3_g[h][:])
+        r1 = tile("r1", [P, PACK, S], F32, "w3_raw")
+        first_remainder(0)
+        first_remainder(1)
         w4_g = weave(w4_raw[:], "w4_g")
-        r1 = tile("r1", [P, PACK, S], F32, "w4_raw")
-        for t in range(PACK):
-            first_remainder(t)
+        first_remainder(2)
+        first_remainder(3)
+        w4_q = quantize(w4_g[:], "w4")
 
         pairs = ((0, 1), (2, 3))
         out_rows = out.rearrange("(m p) j -> p m j", p=P)
         r1_ga = weave(r1[:, :, halves[0]], "r1_ga")
         r1_gb = weave(r1[:, :, halves[1]], "r1_gb")
         r1_qa = quantize(r1_ga[:], "r1_a")
-        r1_qb = quantize(r1_gb[:], "r1_b")
         z_ga = second_remainder(r1[:, :, halves[0]], second[0][:], "z_ga")
-        w4_q = quantize(w4_g[:], "w4", "r1_gb")
+        r1_qb = quantize(r1_gb[:], "r1_b", "r1_ga")
         z_qa = quantize(z_ga[:], "z_a")
         acc_a = [bank(u) for u in range(2)]
         for u in range(2):
             passes(acc_a[u], pairs[u], w3_q, r1_qa, halves[0], True, False)
-        acc_b = [[bank(2 + 2 * i + u) for u in range(2)] for i in range(2)]
-        for i in range(2):
-            for u in range(2):
-                passes(acc_b[i][u], pairs[u], w3_q, r1_qb, rows(i), True, False)
+        acc_third = [bank(2 + u) for u in range(2)]
+        for u in range(2):
+            passes(acc_third[u], pairs[u], w3_q, r1_qb, rows(0), True, False)
+        acc_last = [bank(PACK + m) for m in range(PACK)]
+        for m in range(PACK):
+            passes(acc_last[m], (m,), w3_q, r1_qb, rows(1), True, False)
         for u in range(2):
             passes(acc_a[u], pairs[u], w4_q, z_qa, halves[0], False, True)
             staged = tile("staged%d" % u, [P, 2, HALF], F32, "half_c%d" % (2 + u))
             nc.scalar.copy(staged[:].rearrange("p m j -> p (m j)"), acc_a[u][:])
             nc.sync.dma_start(out_rows[:, 2 * u : 2 * u + 2, halves[0]], staged[:])
 
-        quarters = [slice(HALF + P * i, HALF + P * (i + 1)) for i in range(2)]
-        z_gb = [second_remainder(r1[:, :, quarters[i]], second[1][:, :, rows(i)], "z_gb%d" % i) for i in range(2)]
-        staged_b = [tile("staged_b%d" % u, [P, 2, HALF], F32) for u in range(2)]
-        for i in range(2):
-            z_qb = quantize(z_gb[i][:], "z_b%d" % i)
-            for u, copy in enumerate((nc.scalar.copy, nc.vector.tensor_copy)):
-                passes(acc_b[i][u], pairs[u], w4_q, z_qb, rows(0), False, True)
-                copy(staged_b[u][:, :, rows(i)], acc_b[i][u][:, :HALF].rearrange("p (m j) -> p m j", m=2))
+        z_gb = [second_remainder(r1[:, :, quarters[i]], second[1 + i][:], "z_gb%d" % i) for i in range(2)]
+        staged_b = tile("staged_b", [P, PACK, HALF], F32)
+        copies = (nc.scalar.copy, nc.vector.tensor_copy)
+        z_qb = [quantize(z_gb[i][:], "z_b%d" % i) for i in range(2)]
         for u in range(2):
-            nc.sync.dma_start(out_rows[:, 2 * u : 2 * u + 2, halves[1]], staged_b[u][:])
+            passes(acc_third[u], pairs[u], w4_q, z_qb[0], rows(0), False, True)
+            copies[u](staged_b[:, 2 * u : 2 * u + 2, rows(0)], acc_third[u][:, :HALF].rearrange("p (m j) -> p m j", m=2))
+        for m in range(PACK):
+            passes(acc_last[m], (m,), w4_q, z_qb[1], rows(0), False, True)
+            copies[m % 2](staged_b[:, m, rows(1)], acc_last[m][:, :P])
+            nc.sync.dma_start(out_rows[:, m, halves[1]], staged_b[:, m, :])

@@ -139,14 +139,12 @@ def tile_picked_rvqres_none_p_kernel(
         for t in range(PACK):
             if t:
                 nc.scalar.mul(half_c[t][:], c_acc[t][:], -0.5)
-            for cols in halves if t else (halves[0], rows(2)):
+            for cols in halves:
                 nc.scalar.activation(first[:, t, cols], half_c[t][:].indirect(entries(c1_t, cols)), COPY)
         quarters = [slice(HALF + P * i, HALF + P * (i + 1)) for i in range(2)]
-        second = []
-        for cols, tag in zip([halves[0]] + quarters, ("w2_1_codes", "x_book_codes", "x_book_scales")):
-            second.append(tile("second%d" % cols.start, [P, PACK, cols.stop - cols.start], F32, tag))
-            for t in range(PACK):
-                nc.scalar.activation(second[-1][:, t, :], half_c[t][:].indirect(entries(c2_t, cols)), COPY)
+        second_a = tile("second_a", [P, PACK, HALF], F32, "w2_1_codes")
+        for t in range(PACK):
+            nc.scalar.activation(second_a[:, t, :], half_c[t][:].indirect(entries(c2_t, halves[0])), COPY)
 
         def weave(planes, name):
             grouped = tile(name, [P, PACK * planes.shape[2]], BF16)
@@ -184,7 +182,6 @@ def tile_picked_rvqres_none_p_kernel(
         y_acc = []
         for u in range(2):
             picked_products(u, None)
-        nc.vector.tensor_copy(first[:, 0, rows(3)], half_c[0][:].indirect(entries(c1_t, rows(3))))
         w3_g = [weave(w3_raw[:, :, halves[h]], "w3_g%d" % h) for h in range(2)]
         w3_q = operand("w3", N)
         for h in range(2):
@@ -200,9 +197,15 @@ def tile_picked_rvqres_none_p_kernel(
         pairs = ((0, 1), (2, 3))
         out_rows = out.rearrange("(m p) j -> p m j", p=P)
         r1_ga = weave(r1[:, :, halves[0]], "r1_ga")
-        r1_gb = weave(r1[:, :, halves[1]], "r1_gb")
+        r1_gb = tile("r1_gb", [P, PACK * HALF], BF16)
+        nc.vector.tensor_copy(*woven_views(r1_gb[:, : PACK * P], r1[:, :, quarters[0]]))
+        nc.scalar.copy(*woven_views(r1_gb[:, PACK * P :], r1[:, :, quarters[1]]))
+        second_b = tile("second_b", [P, PACK, HALF], F32, "first")
+        for i in range(2):
+            for t in range(PACK):
+                nc.scalar.activation(second_b[:, t, rows(i)], half_c[t][:].indirect(entries(c2_t, quarters[i])), COPY)
         r1_qa = quantize(r1_ga[:], "r1_a")
-        z_ga = second_remainder(r1[:, :, halves[0]], second[0][:], "z_ga")
+        z_ga = second_remainder(r1[:, :, halves[0]], second_a[:], "z_ga")
         r1_qb = quantize(r1_gb[:], "r1_b", "r1_ga")
         z_qa = quantize(z_ga[:], "z_a")
         acc_a = [bank(u) for u in range(2)]
@@ -220,7 +223,7 @@ def tile_picked_rvqres_none_p_kernel(
             nc.scalar.copy(staged[:].rearrange("p m j -> p (m j)"), acc_a[u][:])
             nc.sync.dma_start(out_rows[:, 2 * u : 2 * u + 2, halves[0]], staged[:])
 
-        z_gb = [second_remainder(r1[:, :, quarters[i]], second[1 + i][:], "z_gb%d" % i) for i in range(2)]
+        z_gb = [second_remainder(r1[:, :, quarters[i]], second_b[:, :, rows(i)], "z_gb%d" % i) for i in range(2)]
         staged_b = tile("staged_b", [P, PACK, HALF], F32)
         copies = (nc.scalar.copy, nc.vector.tensor_copy)
         z_qb = [quantize(z_gb[i][:], "z_b%d" % i) for i in range(2)]

@@ -21,6 +21,7 @@ PACK = 4
 HALF = 256
 SHARE = 80
 LEAD = 384
+ASIDE = 64
 
 
 def tile_picked_rvqres_none_p_kernel(
@@ -198,8 +199,8 @@ def tile_picked_rvqres_none_p_kernel(
         out_rows = out.rearrange("(m p) j -> p m j", p=P)
         r1_ga = weave(r1[:, :, halves[0]], "r1_ga")
         r1_gb = tile("r1_gb", [P, PACK * HALF], BF16)
-        nc.vector.tensor_copy(*woven_views(r1_gb[:, : PACK * P], r1[:, :, quarters[0]]))
-        nc.scalar.copy(*woven_views(r1_gb[:, PACK * P :], r1[:, :, quarters[1]]))
+        nc.vector.tensor_copy(*woven_views(r1_gb[:, : PACK * (HALF - ASIDE)], r1[:, :, HALF : S - ASIDE]))
+        nc.scalar.copy(*woven_views(r1_gb[:, PACK * (HALF - ASIDE) :], r1[:, :, S - ASIDE :]))
         second_b = tile("second_b", [P, PACK, HALF], F32, "first")
         for i in range(2):
             for t in range(PACK):
@@ -211,12 +212,10 @@ def tile_picked_rvqres_none_p_kernel(
         acc_a = [bank(u) for u in range(2)]
         for u in range(2):
             passes(acc_a[u], pairs[u], w3_q, r1_qa, halves[0], True, False)
-        acc_third = [bank(2 + u) for u in range(2)]
-        for u in range(2):
-            passes(acc_third[u], pairs[u], w3_q, r1_qb, rows(0), True, False)
-        acc_last = [bank(PACK + m) for m in range(PACK)]
-        for m in range(PACK):
-            passes(acc_last[m], (m,), w3_q, r1_qb, rows(1), True, False)
+        acc_b = [[bank(2 + 2 * i + u) for u in range(2)] for i in range(2)]
+        for i in range(2):
+            for u in range(2):
+                passes(acc_b[i][u], pairs[u], w3_q, r1_qb, rows(i), True, False)
         for u in range(2):
             passes(acc_a[u], pairs[u], w4_q, z_qa, halves[0], False, True)
             staged = tile("staged%d" % u, [P, 2, HALF], F32, "half_c%d" % (2 + u))
@@ -224,13 +223,11 @@ def tile_picked_rvqres_none_p_kernel(
             nc.sync.dma_start(out_rows[:, 2 * u : 2 * u + 2, halves[0]], staged[:])
 
         z_gb = [second_remainder(r1[:, :, quarters[i]], second_b[:, :, rows(i)], "z_gb%d" % i) for i in range(2)]
-        staged_b = tile("staged_b", [P, PACK, HALF], F32)
-        copies = (nc.scalar.copy, nc.vector.tensor_copy)
-        z_qb = [quantize(z_gb[i][:], "z_b%d" % i) for i in range(2)]
+        staged_b = [tile("staged_b%d" % u, [P, 2, HALF], F32) for u in range(2)]
+        for i in range(2):
+            z_qb = quantize(z_gb[i][:], "z_b%d" % i)
+            for u, copy in enumerate((nc.scalar.copy, nc.vector.tensor_copy)):
+                passes(acc_b[i][u], pairs[u], w4_q, z_qb, rows(0), False, True)
+                copy(staged_b[u][:, :, rows(i)], acc_b[i][u][:, :HALF].rearrange("p (m j) -> p m j", m=2))
         for u in range(2):
-            passes(acc_third[u], pairs[u], w4_q, z_qb[0], rows(0), False, True)
-            copies[u](staged_b[:, 2 * u : 2 * u + 2, rows(0)], acc_third[u][:, :HALF].rearrange("p (m j) -> p m j", m=2))
-        for m in range(PACK):
-            passes(acc_last[m], (m,), w4_q, z_qb[1], rows(0), False, True)
-            copies[m % 2](staged_b[:, m, rows(1)], acc_last[m][:, :P])
-            nc.sync.dma_start(out_rows[:, m, halves[1]], staged_b[:, m, :])
+            nc.sync.dma_start(out_rows[:, 2 * u : 2 * u + 2, halves[1]], staged_b[u][:])

@@ -101,9 +101,9 @@ def tile_picked_rvqres_none_p_kernel(
         w2_raw = load_weight(w2, "w2_raw")
         c1_t = load_list(c1, "c1_t")
         w1_raw = load_weight(w1, "w1_raw")
-        c2_t = load_list(c2, "c2_t")
         w3_raw = load_weight(w3, "w3_raw")
         w4_raw = load_weight(w4, "w4_raw")
+        c2_t = load_list(c2, "c2_t")
 
         x_book = operand("x_book", V)
         pick_scales = tile("pick_scales", [P, S], U8)
@@ -140,7 +140,7 @@ def tile_picked_rvqres_none_p_kernel(
         for t in range(PACK):
             if t:
                 nc.scalar.mul(half_c[t][:], c_acc[t][:], -0.5)
-            for cols in halves:
+            for cols in halves if t else (halves[0], rows(2)):
                 nc.scalar.activation(first[:, t, cols], half_c[t][:].indirect(entries(c1_t, cols)), COPY)
         quarters = [slice(HALF + P * i, HALF + P * (i + 1)) for i in range(2)]
         second_a = tile("second_a", [P, PACK, HALF], F32, "w2_1_codes")
@@ -158,14 +158,16 @@ def tile_picked_rvqres_none_p_kernel(
             nc.vector.tensor_tensor(dst, src, woven_views(z_g[:], found)[1], ADD)
             return z_g
 
-        def picked_products(u, tag):
-            w1_q = quantize(w1_g[u][:], "w1_%d" % u, tag)
-            for e in range(2):
-                y_acc.append(bank(PACK + 2 * u + e))
-                product(y_acc[-1][:, :P], w1_q, rows(e), (early_words, pick_scales), rows(0), True, True)
-                late = (late_words, pick_scales[:, P:])
-                product(y_acc[-1][:, P:HALF], w1_q, rows(e), late, rows(0), True, True)
-                product(y_acc[-1][:, HALF:], w1_q, rows(e), late, slice(P, S - P), True, True)
+        def quantize_half(into, h, grouped):
+            nc.vector.quantize_mx(out=into[0][:, halves[h]].bitcast(FP8X4), scales=into[1][:, halves[h]], in_=grouped)
+
+        def picked_product(t):
+            acc = bank(PACK + t)
+            late = (late_words, pick_scales[:, P:])
+            product(acc[:, :P], w1_q, rows(t), (early_words, pick_scales), rows(0), True, True)
+            product(acc[:, P:HALF], w1_q, rows(t), late, rows(0), True, True)
+            product(acc[:, HALF:], w1_q, rows(t), late, slice(P, S - P), True, True)
+            return acc
 
         def first_remainder(t):
             nc.vector.scalar_tensor_tensor(r1[:, t, :], first[:, t, :], 2.0, y_acc[t][:], MULT, ADD)
@@ -177,29 +179,31 @@ def tile_picked_rvqres_none_p_kernel(
                     acc[:, count * i : count * (i + 1)], left, rows(m), right, cols, start and i == 0, stop and i == len(ms) - 1
                 )
 
-        w1_g = [tile("w1_g%d" % u, [P, 2 * H], BF16) for u in range(2)]
-        for u in range(2):
-            nc.vector.tensor_copy(*dealt_views(w1_g[u][:], w1_raw, u))
-        y_acc = []
-        for u in range(2):
-            picked_products(u, None)
+        w1_g = tile("w1_g", [P, PACK * H], BF16)
+        nc.vector.tensor_copy(
+            w1_g[:].rearrange("p (t m j) -> p m j t", t=PACK, j=PACK), w1_raw[:].rearrange("p j (m t) -> p m j t", t=PACK)
+        )
+        nc.vector.tensor_copy(first[:, 0, rows(3)], half_c[0][:].indirect(entries(c1_t, rows(3))))
+        w1_q = quantize(w1_g[:], "w1")
+        y_acc = [picked_product(t) for t in range(PACK)]
         w3_g = [weave(w3_raw[:, :, halves[h]], "w3_g%d" % h) for h in range(2)]
         w3_q = operand("w3", N)
         for h in range(2):
-            nc.vector.quantize_mx(out=w3_q[0][:, halves[h]].bitcast(FP8X4), scales=w3_q[1][:, halves[h]], in_=w3_g[h][:])
+            quantize_half(w3_q, h, w3_g[h][:])
         r1 = tile("r1", [P, PACK, S], F32, "w3_raw")
         first_remainder(0)
         first_remainder(1)
         w4_g = weave(w4_raw[:], "w4_g")
         first_remainder(2)
         first_remainder(3)
-        w4_q = quantize(w4_g[:], "w4")
+        w4_q = operand("w4", N)
+        quantize_half(w4_q, 0, w4_g[:, : PACK * HALF])
+        r1_ga = weave(r1[:, :, halves[0]], "r1_ga")
+        quantize_half(w4_q, 1, w4_g[:, PACK * HALF :])
 
         pairs = ((0, 1), (2, 3))
         out_rows = out.rearrange("(m p) j -> p m j", p=P)
-        r1_ga = weave(r1[:, :, halves[0]], "r1_ga")
         r1_gb = tile("r1_gb", [P, PACK * HALF], BF16)
-        nc.vector.tensor_copy(*woven_views(r1_gb[:, : PACK * (HALF - ASIDE)], r1[:, :, HALF : S - ASIDE]))
         nc.scalar.copy(*woven_views(r1_gb[:, PACK * (HALF - ASIDE) :], r1[:, :, S - ASIDE :]))
         second_b = tile("second_b", [P, PACK, HALF], F32, "first")
         for i in range(2):
@@ -207,21 +211,22 @@ def tile_picked_rvqres_none_p_kernel(
                 nc.scalar.activation(second_b[:, t, rows(i)], half_c[t][:].indirect(entries(c2_t, quarters[i])), COPY)
         r1_qa = quantize(r1_ga[:], "r1_a")
         z_ga = second_remainder(r1[:, :, halves[0]], second_a[:], "z_ga")
-        r1_qb = quantize(r1_gb[:], "r1_b", "r1_ga")
+        nc.vector.tensor_copy(*woven_views(r1_gb[:, : PACK * (HALF - ASIDE)], r1[:, :, HALF : S - ASIDE]))
         z_qa = quantize(z_ga[:], "z_a")
+        r1_qb = quantize(r1_gb[:], "r1_b")
         acc_a = [bank(u) for u in range(2)]
         for u in range(2):
             passes(acc_a[u], pairs[u], w3_q, r1_qa, halves[0], True, False)
-        acc_b = [[bank(2 + 2 * i + u) for u in range(2)] for i in range(2)]
-        for i in range(2):
-            for u in range(2):
-                passes(acc_b[i][u], pairs[u], w3_q, r1_qb, rows(i), True, False)
         for u in range(2):
             passes(acc_a[u], pairs[u], w4_q, z_qa, halves[0], False, True)
             staged = tile("staged%d" % u, [P, 2, HALF], F32, "half_c%d" % (2 + u))
             nc.scalar.copy(staged[:].rearrange("p m j -> p (m j)"), acc_a[u][:])
             nc.sync.dma_start(out_rows[:, 2 * u : 2 * u + 2, halves[0]], staged[:])
 
+        acc_b = [[bank(2 + 2 * i + u) for u in range(2)] for i in range(2)]
+        for i in range(2):
+            for u in range(2):
+                passes(acc_b[i][u], pairs[u], w3_q, r1_qb, rows(i), True, False)
         z_gb = [second_remainder(r1[:, :, quarters[i]], second_b[:, :, rows(i)], "z_gb%d" % i) for i in range(2)]
         staged_b = [tile("staged_b%d" % u, [P, 2, HALF], F32) for u in range(2)]
         for i in range(2):

@@ -22,6 +22,7 @@ HALF = 256
 SHARE = 80
 LEAD = 384
 ASIDE = 64
+POOL = 384
 
 
 def tile_picked_rvqres_none_p_kernel(
@@ -31,6 +32,7 @@ def tile_picked_rvqres_none_p_kernel(
     with ExitStack() as ctx:
         lists = ctx.enter_context(tc.tile_pool(name="lists", bufs=1))
         keep = ctx.enter_context(tc.tile_pool(name="keep", bufs=1))
+        reuse = ctx.enter_context(tc.tile_pool(name="reuse", bufs=1))
         psum = ctx.enter_context(tc.psum_pool(name="psum", bufs=1))
 
         def tile(name, shape, dtype, tag=None):
@@ -136,11 +138,11 @@ def tile_picked_rvqres_none_p_kernel(
         for t in range(1, PACK):
             product(c_acc[t][:], w2_q[t // 2], rows(t % 2), x_book, whole, True, True)
 
-        first = tile("first", [P, PACK, S], F32)
+        first = reuse.tile([P, PACK, S], F32, name="first", offset=4096, align_bytes=64)
         for t in range(PACK):
             if t:
                 nc.scalar.mul(half_c[t][:], c_acc[t][:], -0.5)
-            for cols in halves if t else (halves[0], rows(2)):
+            for cols in ((halves[0], rows(2)), halves, halves, halves[:1])[t]:
                 nc.scalar.activation(first[:, t, cols], half_c[t][:].indirect(entries(c1_t, cols)), COPY)
         quarters = [slice(HALF + P * i, HALF + P * (i + 1)) for i in range(2)]
         second_a = tile("second_a", [P, PACK, HALF], F32, "w2_1_codes")
@@ -186,26 +188,33 @@ def tile_picked_rvqres_none_p_kernel(
         nc.vector.tensor_copy(first[:, 0, rows(3)], half_c[0][:].indirect(entries(c1_t, rows(3))))
         w1_q = quantize(w1_g[:], "w1")
         y_acc = [picked_product(t) for t in range(PACK)]
-        w3_g = [weave(w3_raw[:, :, halves[h]], "w3_g%d" % h) for h in range(2)]
+        w3_g = [reuse.tile([P, PACK * HALF], BF16, name="w3_g%d" % h, offset=2048 * h, align_bytes=64) for h in range(2)]
+        for h in range(2):
+            nc.vector.tensor_copy(*woven_views(w3_g[h][:], w3_raw[:, :, halves[h]]))
         w3_q = operand("w3", N)
         for h in range(2):
             quantize_half(w3_q, h, w3_g[h][:])
         r1 = tile("r1", [P, PACK, S], F32, "w3_raw")
-        first_remainder(0)
-        first_remainder(1)
-        w4_g = weave(w4_raw[:], "w4_g")
-        first_remainder(2)
-        first_remainder(3)
-        w4_q = operand("w4", N)
-        quantize_half(w4_q, 0, w4_g[:, : PACK * HALF])
+        w4_ga = reuse.tile([P, POOL, PACK], BF16, name="w4_ga", offset=0, align_bytes=64)
+        nc.gpsimd.tensor_scalar(w4_ga[:], w4_raw[:, :, :POOL].rearrange("p t c -> p c t"), 1.0, 0.0, MULT, ADD)
+        for t in range(3):
+            first_remainder(t)
+        first_b = reuse.tile([P, HALF], F32, name="first_b", offset=3072, align_bytes=64)
+        nc.vector.tensor_copy(first_b[:], half_c[3][:].indirect(entries(c1_t, halves[1])))
+        for cols, found in zip(halves, (first[:, 3, halves[0]], first_b[:])):
+            nc.vector.scalar_tensor_tensor(r1[:, 3, cols], found, 2.0, y_acc[3][:, cols], MULT, ADD)
+        w4_gb = reuse.tile([P, PACK * (N - POOL)], BF16, name="w4_gb", offset=8192, align_bytes=64)
+        nc.vector.tensor_copy(*woven_views(w4_gb[:], w4_raw[:, :, POOL:]))
         r1_ga = weave(r1[:, :, halves[0]], "r1_ga")
-        quantize_half(w4_q, 1, w4_g[:, PACK * HALF :])
+        w4_q = operand("w4", N)
+        for cols, grouped in ((slice(POOL, N), w4_gb[:]), (slice(0, POOL), w4_ga[:].rearrange("p c t -> p (c t)"))):
+            nc.vector.quantize_mx(out=w4_q[0][:, cols].bitcast(FP8X4), scales=w4_q[1][:, cols], in_=grouped)
 
         pairs = ((0, 1), (2, 3))
         out_rows = out.rearrange("(m p) j -> p m j", p=P)
         r1_gb = tile("r1_gb", [P, PACK * HALF], BF16)
         nc.scalar.copy(*woven_views(r1_gb[:, PACK * (HALF - ASIDE) :], r1[:, :, S - ASIDE :]))
-        second_b = tile("second_b", [P, PACK, HALF], F32, "first")
+        second_b = reuse.tile([P, PACK, HALF], F32, name="second_b", offset=4096, align_bytes=64)
         for i in range(2):
             for t in range(PACK):
                 nc.scalar.activation(second_b[:, t, rows(i)], half_c[t][:].indirect(entries(c2_t, quarters[i])), COPY)

@@ -33,6 +33,7 @@ def tile_picked_rvqres_none_p_kernel(
         lists = ctx.enter_context(tc.tile_pool(name="lists", bufs=1))
         keep = ctx.enter_context(tc.tile_pool(name="keep", bufs=1))
         reuse = ctx.enter_context(tc.tile_pool(name="reuse", bufs=1))
+        held = ctx.enter_context(tc.tile_pool(name="held", bufs=1))
         psum = ctx.enter_context(tc.psum_pool(name="psum", bufs=1))
 
         def tile(name, shape, dtype, tag=None):
@@ -43,10 +44,16 @@ def tile_picked_rvqres_none_p_kernel(
             nc.sync.dma_start(offsets[:], src)
             return offsets
 
-        def load_weight(w, name):
-            raw = tile(name, [P, PACK, w.shape[1]], F32)
+        def placed(name, shape, dtype, offset):
+            return held.tile(shape, dtype, name=name, offset=offset, align_bytes=64)
+
+        def load_weight(w, raw):
             nc.sync.dma_start(raw[:], w.rearrange("(p j) n -> p j n", j=PACK))
             return raw
+
+        def move_rows(planes, found):
+            for r in range(4):
+                nc.sync.dma_start(planes[r:P:32, :].bitcast(I32), found[8 * r : P : 32, :].bitcast(I32))
 
         def operand(name, width, tag=None):
             return tile(name + "_codes", [P, width], U32, tag), tile(name + "_scales", [P, width], U8)
@@ -90,27 +97,34 @@ def tile_picked_rvqres_none_p_kernel(
 
         halves = [slice(h * HALF, (h + 1) * HALF) for h in range(2)]
         whole = slice(0, 512)
-        x_bytes = tile("x_bytes", [P, T], U8)
+        raw_shape, raw_bytes = [P, PACK, 512], 8192
+        x_bytes = placed("x_bytes", [P, T], U8, raw_bytes - T // 2)
         nc.vector.memset(x_bytes[:].bitcast(I32), 0)
+        book_scales = tile("book_scales", [P, V], U8)
+        pick_scales = tile("pick_scales", [P, S], U8)
+        for planes in (book_scales, pick_scales):
+            nc.vector.memset(planes[:].bitcast(I32), 0)
         x_table = tile("x_table", [P, T], I32)
         x_rows = x_words[0].rearrange("p n t -> p (n t)").bitcast(I32)
         nc.sync.dma_start(x_table[:, :LEAD], x_rows[:, :LEAD])
         book_t = load_list(book, "book_t")
         offs_t = load_list(offs, "offs_t")
-        for r in range(4):
-            nc.sync.dma_start(x_bytes[r:P:32, :].bitcast(I32), x_scales[0, r:16:4, :].bitcast(I32))
+        nc.sync.dma_start(x_bytes[0:P:8, :].bitcast(I32), x_scales[0].bitcast(I32))
         nc.sync.dma_start(x_table[:, LEAD:], x_rows[:, LEAD:])
-        w2_raw = load_weight(w2, "w2_raw")
+        w2_raw = load_weight(w2, tile("w2_raw", raw_shape, F32))
         c1_t = load_list(c1, "c1_t")
-        w1_raw = load_weight(w1, "w1_raw")
-        w3_raw = load_weight(w3, "w3_raw")
-        w4_raw = load_weight(w4, "w4_raw")
         c2_t = load_list(c2, "c2_t")
 
-        x_book = operand("x_book", V)
-        pick_scales = tile("pick_scales", [P, S], U8)
-        nc.vector.tensor_copy(x_book[1][:], x_bytes[:].indirect(book_t[:]))
-        nc.vector.tensor_copy(pick_scales[:], x_bytes[:].indirect(offs_t[:]))
+        book_bytes = placed("book_bytes", [P, V], U8, 2 * raw_bytes)
+        pick_bytes = tile("pick_bytes", [P, S], U8)
+        nc.vector.tensor_copy(book_bytes[:], x_bytes[:].indirect(book_t[:]))
+        nc.vector.tensor_copy(pick_bytes[:], x_bytes[:].indirect(offs_t[:]))
+        move_rows(book_scales, book_bytes)
+        w1_raw = load_weight(w1, placed("w1_raw", raw_shape, F32, 0))
+        move_rows(pick_scales, pick_bytes)
+        w3_raw = load_weight(w3, placed("w3_raw", raw_shape, F32, raw_bytes))
+        w4_raw = load_weight(w4, placed("w4_raw", raw_shape, F32, 2 * raw_bytes))
+        x_book = (tile("book_words", [P, V], U32), book_scales)
         nc.vector.tensor_copy(x_book[0][:], x_table[:].bitcast(U32).indirect(book_t[:]))
 
         early_words = tile("early_words", [P, P], U32)
@@ -194,7 +208,7 @@ def tile_picked_rvqres_none_p_kernel(
         w3_q = operand("w3", N)
         for h in range(2):
             quantize_half(w3_q, h, w3_g[h][:])
-        r1 = tile("r1", [P, PACK, S], F32, "w3_raw")
+        r1 = placed("r1", [P, PACK, S], F32, raw_bytes)
         w4_ga = reuse.tile([P, POOL, PACK], BF16, name="w4_ga", offset=0, align_bytes=64)
         nc.gpsimd.tensor_scalar(w4_ga[:], w4_raw[:, :, :POOL].rearrange("p t c -> p c t"), 1.0, 0.0, MULT, ADD)
         for t in range(3):

@@ -51,9 +51,9 @@ def tile_picked_rvqres_none_p_kernel(
             nc.sync.dma_start(raw[:], w.rearrange("(p j) n -> p j n", j=PACK))
             return raw
 
-        def move_rows(planes, found):
+        def move_rows(planes, start, found):
             for r in range(4):
-                nc.sync.dma_start(planes[r:P:32, :].bitcast(I32), found[8 * r : P : 32, :].bitcast(I32))
+                nc.sync.dma_start(planes[start + r : P : 32, :].bitcast(I32), found[48 + r : 64 : 4, :].bitcast(I32))
 
         def operand(name, width, tag=None):
             return tile(name + "_codes", [P, width], U32, tag), tile(name + "_scales", [P, width], U8)
@@ -99,7 +99,8 @@ def tile_picked_rvqres_none_p_kernel(
         whole = slice(0, 512)
         raw_shape, raw_bytes = [P, PACK, 512], 8192
         x_bytes = placed("x_bytes", [P, T], U8, raw_bytes - T // 2)
-        nc.vector.memset(x_bytes[:].bitcast(I32), 0)
+        for unloaded in (slice(0, 48), slice(64, P)):
+            nc.vector.memset(x_bytes[unloaded, :].bitcast(I32), 0)
         book_scales = tile("book_scales", [P, V], U8)
         pick_scales = tile("pick_scales", [P, S], U8)
         for planes in (book_scales, pick_scales):
@@ -108,8 +109,8 @@ def tile_picked_rvqres_none_p_kernel(
         x_rows = x_words[0].rearrange("p n t -> p (n t)").bitcast(I32)
         nc.sync.dma_start(x_table[:, :LEAD], x_rows[:, :LEAD])
         book_t = load_list(book, "book_t")
+        nc.sync.dma_start(x_bytes[48:64, :].bitcast(I32), x_scales[0].bitcast(I32))
         offs_t = load_list(offs, "offs_t")
-        nc.sync.dma_start(x_bytes[0:P:8, :].bitcast(I32), x_scales[0].bitcast(I32))
         nc.sync.dma_start(x_table[:, LEAD:], x_rows[:, LEAD:])
         w2_raw = load_weight(w2, tile("w2_raw", raw_shape, F32))
         c1_t = load_list(c1, "c1_t")
@@ -119,9 +120,9 @@ def tile_picked_rvqres_none_p_kernel(
         pick_bytes = tile("pick_bytes", [P, S], U8)
         nc.vector.tensor_copy(book_bytes[:], x_bytes[:].indirect(book_t[:]))
         nc.vector.tensor_copy(pick_bytes[:], x_bytes[:].indirect(offs_t[:]))
-        move_rows(book_scales, book_bytes)
+        move_rows(book_scales, 0, book_bytes)
         w1_raw = load_weight(w1, placed("w1_raw", raw_shape, F32, 0))
-        move_rows(pick_scales, pick_bytes)
+        move_rows(pick_scales, 4, pick_bytes)
         w3_raw = load_weight(w3, placed("w3_raw", raw_shape, F32, raw_bytes))
         w4_raw = load_weight(w4, placed("w4_raw", raw_shape, F32, 2 * raw_bytes))
         x_book = (tile("book_words", [P, V], U32), book_scales)
@@ -179,8 +180,8 @@ def tile_picked_rvqres_none_p_kernel(
 
         def picked_product(t):
             acc = bank(PACK + t)
-            late = (late_words, pick_scales[:, P:])
-            product(acc[:, :P], w1_q, rows(t), (early_words, pick_scales), rows(0), True, True)
+            late = (late_words, pick_scales[4:, P:])
+            product(acc[:, :P], w1_q, rows(t), (early_words, pick_scales[4:, :]), rows(0), True, True)
             product(acc[:, P:HALF], w1_q, rows(t), late, rows(0), True, True)
             product(acc[:, HALF:], w1_q, rows(t), late, slice(P, S - P), True, True)
             return acc

from contextlib import ExitStack

import concourse.mybir as mybir

K, T, S, V, N, H = 512, 2048, 512, 512, 512, 512
FLOPS = 2 * K * H * S + 2 * K * H * V + 2 * 2 * H * N * S

F32 = mybir.dt.float32
BF16 = mybir.dt.bfloat16
I32 = mybir.dt.int32
U32 = mybir.dt.uint32
U16 = mybir.dt.uint16
U8 = mybir.dt.uint8
FP8X4 = mybir.dt.float8_e4m3fn_x4
ADD = mybir.AluOpType.add
MULT = mybir.AluOpType.mult
COPY = mybir.ActivationFunctionType.Copy

P = 128
PACK = 4
HALF = 256
SHARE = 80
LEAD = 384
ASIDE = 64
POOL = 384


def tile_picked_rvqres_none_p_kernel(
    tc, x_words, x_scales, w1, w2, w3, w4, offs, book, c1, c2, out
):
    nc = tc.nc
    with ExitStack() as ctx:
        lists = ctx.enter_context(tc.tile_pool(name="lists", bufs=1))
        keep = ctx.enter_context(tc.tile_pool(name="keep", bufs=1))
        reuse = ctx.enter_context(tc.tile_pool(name="reuse", bufs=1))
        held = ctx.enter_context(tc.tile_pool(name="held", bufs=1))
        psum = ctx.enter_context(tc.psum_pool(name="psum", bufs=1))

        def tile(name, shape, dtype, tag=None):
            return keep.tile(shape, dtype, name=name, tag=tag or name, align_bytes=64)

        def load_list(src, name):
            offsets = lists.tile([P, S // 16], U16, name=name)
            nc.sync.dma_start(offsets[:], src)
            return offsets

        def placed(name, shape, dtype, offset):
            return held.tile(shape, dtype, name=name, offset=offset, align_bytes=64)

        def load_weight(w, raw):
            nc.sync.dma_start(raw[:], w.rearrange("(p j) n -> p j n", j=PACK))
            return raw

        def move_rows(planes, start, found):
            for r in range(4):
                nc.sync.dma_start(planes[start + r : P : 32, :].bitcast(I32), found[48 + r : 64 : 4, :].bitcast(I32))

        def operand(name, width, tag=None):
            return tile(name + "_codes", [P, width], U32, tag), tile(name + "_scales", [P, width], U8)

        def quantize(grouped, name, tag=None):
            codes, scales = operand(name, grouped.shape[1] // PACK, tag)
            nc.vector.quantize_mx(out=codes[:].bitcast(FP8X4), scales=scales[:], in_=grouped)
            return codes, scales

        def product(acc, left, cols, right, right_cols, start, stop):
            nc.tensor.matmul_mx(
                out=acc,
                lhsT=left[0][:, cols].bitcast(FP8X4),
                lhsT_scale=left[1][:, cols],
                rhs=right[0][:, right_cols].bitcast(FP8X4),
                rhs_scale=right[1][:, right_cols],
                start=start,
                stop=stop,
            )

        def dealt_views(grouped, raw, u):
            return (
                grouped.rearrange("p (t m j) -> p m j t", t=2, j=PACK),
                raw[:].rearrange("p j (m t) -> p m j t", t=PACK)[:, :, :, 2 * u : 2 * u + 2],
            )

        def woven_views(grouped, planes):
            return (
                grouped.rearrange("p (c i t) -> p c t i", t=PACK, i=4),
                planes.rearrange("p t (c i) -> p c t i", i=4),
            )

        def bank(b):
            return psum.tile([P, 512], F32, name="bank%d" % b)

        def rows(t):
            return slice(P * t, P * (t + 1))

        def entries(offsets, cols):
            return offsets[:, cols.start // 16 : cols.stop // 16]

        halves = [slice(h * HALF, (h + 1) * HALF) for h in range(2)]
        whole = slice(0, 512)
        raw_shape, raw_bytes = [P, PACK, 512], 8192
        x_bytes = placed("x_bytes", [P, T], U8, raw_bytes - T // 2)
        for unloaded in (slice(0, 48), slice(64, P)):
            nc.vector.memset(x_bytes[unloaded, :].bitcast(I32), 0)
        book_scales = tile("book_scales", [P, V], U8)
        pick_scales = tile("pick_scales", [P, S], U8)
        for planes in (book_scales, pick_scales):
            nc.vector.memset(planes[:].bitcast(I32), 0)
        x_table = tile("x_table", [P, T], I32)
        x_rows = x_words[0].rearrange("p n t -> p (n t)").bitcast(I32)
        nc.sync.dma_start(x_table[:, :LEAD], x_rows[:, :LEAD])
        book_t = load_list(book, "book_t")
        nc.sync.dma_start(x_bytes[48:64, :].bitcast(I32), x_scales[0].bitcast(I32))
        offs_t = load_list(offs, "offs_t")
        nc.sync.dma_start(x_table[:, LEAD:], x_rows[:, LEAD:])
        w2_raw = load_weight(w2, tile("w2_raw", raw_shape, F32))
        c1_t = load_list(c1, "c1_t")
        c2_t = load_list(c2, "c2_t")

        book_bytes = placed("book_bytes", [P, V], U8, 2 * raw_bytes)
        pick_bytes = tile("pick_bytes", [P, S], U8)
        nc.vector.tensor_copy(book_bytes[:], x_bytes[:].indirect(book_t[:]))
        nc.vector.tensor_copy(pick_bytes[:], x_bytes[:].indirect(offs_t[:]))
        move_rows(book_scales, 0, book_bytes)
        w1_raw = load_weight(w1, placed("w1_raw", raw_shape, F32, 0))
        move_rows(pick_scales, 4, pick_bytes)
        w3_raw = load_weight(w3, placed("w3_raw", raw_shape, F32, raw_bytes))
        w4_raw = load_weight(w4, placed("w4_raw", raw_shape, F32, 2 * raw_bytes))
        x_book = (tile("book_words", [P, V], U32), book_scales)
        nc.vector.tensor_copy(x_book[0][:], x_table[:].bitcast(U32).indirect(book_t[:]))

        early_words = tile("early_words", [P, P], U32)
        nc.vector.tensor_copy(early_words[:], x_table[:].bitcast(U32).indirect(entries(offs_t, rows(0))))
        w2_g = [tile("w2_g%d" % u, [P, 2 * H], BF16) for u in range(2)]
        for u, share in enumerate((SHARE, P - SHARE)):
            dst, src = dealt_views(w2_g[u][:], w2_raw, u)
            nc.vector.tensor_copy(dst[:, :share], src[:, :share])
            nc.scalar.copy(dst[:, share:], src[:, share:])
        w2_q = [operand("w2_0", HALF)]
        for t in range(2):
            nc.vector.quantize_mx(
                out=w2_q[0][0][:, rows(t)].bitcast(FP8X4), scales=w2_q[0][1][:, rows(t)], in_=w2_g[0][:, H * t : H * (t + 1)]
            )
        late_words = tile("late_words", [P, S - P], U32, "w2_g0")
        nc.vector.tensor_copy(late_words[:], x_table[:].bitcast(U32).indirect(entries(offs_t, slice(P, S))))
        w2_q.append(quantize(w2_g[1][:], "w2_1"))

        half_c = [tile("half_c%d" % t, [P, V], F32) for t in range(PACK)]
        for i in range(PACK):
            first_acc = bank(PACK + i)
            product(first_acc[:, :P], w2_q[0], rows(0), x_book, rows(i), True, True)
            nc.scalar.mul(half_c[0][:, rows(i)], first_acc[:, :P], -0.5)
        c_acc = [None] + [bank(t) for t in range(1, PACK)]
        for t in range(1, PACK):
            product(c_acc[t][:], w2_q[t // 2], rows(t % 2), x_book, whole, True, True)

        first = reuse.tile([P, PACK, S], F32, name="first", offset=4096, align_bytes=64)
        for t in range(PACK):
            if t:
                nc.scalar.mul(half_c[t][:], c_acc[t][:], -0.5)
            for cols in ((halves[0], rows(2)), halves, halves, halves[:1])[t]:
                nc.scalar.activation(first[:, t, cols], half_c[t][:].indirect(entries(c1_t, cols)), COPY)
        quarters = [slice(HALF + P * i, HALF + P * (i + 1)) for i in range(2)]
        second_a = tile("second_a", [P, PACK, HALF], F32, "w2_1_codes")
        for t in range(PACK):
            nc.scalar.activation(second_a[:, t, :], half_c[t][:].indirect(entries(c2_t, halves[0])), COPY)

        def weave(planes, name):
            grouped = tile(name, [P, PACK * planes.shape[2]], BF16)
            nc.vector.tensor_copy(*woven_views(grouped[:], planes))
            return grouped

        def second_remainder(planes, found, name):
            z_g = tile(name, [P, PACK * planes.shape[2]], BF16)
            dst, src = woven_views(z_g[:], planes)
            nc.vector.tensor_tensor(dst, src, woven_views(z_g[:], found)[1], ADD)
            return z_g

        def quantize_half(into, h, grouped):
            nc.vector.quantize_mx(out=into[0][:, halves[h]].bitcast(FP8X4), scales=into[1][:, halves[h]], in_=grouped)

        def picked_product(t):
            acc = bank(PACK + t)
            late = (late_words, pick_scales[4:, P:])
            product(acc[:, :P], w1_q, rows(t), (early_words, pick_scales[4:, :]), rows(0), True, True)
            product(acc[:, P:HALF], w1_q, rows(t), late, rows(0), True, True)
            product(acc[:, HALF:], w1_q, rows(t), late, slice(P, S - P), True, True)
            return acc

        def first_remainder(t):
            nc.vector.scalar_tensor_tensor(r1[:, t, :], first[:, t, :], 2.0, y_acc[t][:], MULT, ADD)

        def passes(acc, ms, left, right, cols, start, stop):
            count = cols.stop - cols.start
            for i, m in enumerate(ms):
                product(
                    acc[:, count * i : count * (i + 1)], left, rows(m), right, cols, start and i == 0, stop and i == len(ms) - 1
                )

        w1_g = tile("w1_g", [P, PACK * H], BF16)
        nc.vector.tensor_copy(
            w1_g[:].rearrange("p (t m j) -> p m j t", t=PACK, j=PACK), w1_raw[:].rearrange("p j (m t) -> p m j t", t=PACK)
        )
        nc.vector.tensor_copy(first[:, 0, rows(3)], half_c[0][:].indirect(entries(c1_t, rows(3))))
        w1_q = quantize(w1_g[:], "w1")
        y_acc = [picked_product(t) for t in range(PACK)]
        w3_g = [reuse.tile([P, PACK * HALF], BF16, name="w3_g%d" % h, offset=2048 * h, align_bytes=64) for h in range(2)]
        for h in range(2):
            nc.vector.tensor_copy(*woven_views(w3_g[h][:], w3_raw[:, :, halves[h]]))
        w3_q = operand("w3", N)
        for h in range(2):
            quantize_half(w3_q, h, w3_g[h][:])
        r1 = placed("r1", [P, PACK, S], F32, raw_bytes)
        w4_ga = reuse.tile([P, POOL, PACK], BF16, name="w4_ga", offset=0, align_bytes=64)
        nc.gpsimd.tensor_scalar(w4_ga[:], w4_raw[:, :, :POOL].rearrange("p t c -> p c t"), 1.0, 0.0, MULT, ADD)
        for t in range(3):
            first_remainder(t)
        first_b = reuse.tile([P, HALF], F32, name="first_b", offset=3072, align_bytes=64)
        nc.vector.tensor_copy(first_b[:], half_c[3][:].indirect(entries(c1_t, halves[1])))
        for cols, found in zip(halves, (first[:, 3, halves[0]], first_b[:])):
            nc.vector.scalar_tensor_tensor(r1[:, 3, cols], found, 2.0, y_acc[3][:, cols], MULT, ADD)
        w4_gb = reuse.tile([P, PACK * (N - POOL)], BF16, name="w4_gb", offset=8192, align_bytes=64)
        nc.vector.tensor_copy(*woven_views(w4_gb[:], w4_raw[:, :, POOL:]))
        r1_ga = weave(r1[:, :, halves[0]], "r1_ga")
        w4_q = operand("w4", N)
        for cols, grouped in ((slice(POOL, N), w4_gb[:]), (slice(0, POOL), w4_ga[:].rearrange("p c t -> p (c t)"))):
            nc.vector.quantize_mx(out=w4_q[0][:, cols].bitcast(FP8X4), scales=w4_q[1][:, cols], in_=grouped)

        pairs = ((0, 1), (2, 3))
        out_rows = out.rearrange("(m p) j -> p m j", p=P)
        r1_gb = tile("r1_gb", [P, PACK * HALF], BF16)
        nc.scalar.copy(*woven_views(r1_gb[:, PACK * (HALF - ASIDE) :], r1[:, :, S - ASIDE :]))
        second_b = reuse.tile([P, PACK, HALF], F32, name="second_b", offset=4096, align_bytes=64)
        for i in range(2):
            for t in range(PACK):
                nc.scalar.activation(second_b[:, t, rows(i)], half_c[t][:].indirect(entries(c2_t, quarters[i])), COPY)
        r1_qa = quantize(r1_ga[:], "r1_a")
        z_ga = second_remainder(r1[:, :, halves[0]], second_a[:], "z_ga")
        nc.vector.tensor_copy(*woven_views(r1_gb[:, : PACK * (HALF - ASIDE)], r1[:, :, HALF : S - ASIDE]))
        z_qa = quantize(z_ga[:], "z_a")
        r1_qb = quantize(r1_gb[:], "r1_b")
        acc_a = [bank(u) for u in range(2)]
        for u in range(2):
            passes(acc_a[u], pairs[u], w3_q, r1_qa, halves[0], True, False)
        for u in range(2):
            passes(acc_a[u], pairs[u], w4_q, z_qa, halves[0], False, True)
            staged = tile("staged%d" % u, [P, 2, HALF], F32, "half_c%d" % (2 + u))
            nc.scalar.copy(staged[:].rearrange("p m j -> p (m j)"), acc_a[u][:])
            nc.sync.dma_start(out_rows[:, 2 * u : 2 * u + 2, halves[0]], staged[:])

        acc_b = [[bank(2 + 2 * i + u) for u in range(2)] for i in range(2)]
        for i in range(2):
            for u in range(2):
                passes(acc_b[i][u], pairs[u], w3_q, r1_qb, rows(i), True, False)
        z_gb = [second_remainder(r1[:, :, quarters[i]], second_b[:, :, rows(i)], "z_gb%d" % i) for i in range(2)]
        staged_b = [tile("staged_b%d" % u, [P, 2, HALF], F32) for u in range(2)]
        for i in range(2):
            z_qb = quantize(z_gb[i][:], "z_b%d" % i)
            for u, copy in enumerate((nc.scalar.copy, nc.vector.tensor_copy)):
                passes(acc_b[i][u], pairs[u], w4_q, z_qb, rows(0), False, True)
                copy(staged_b[u][:, :, rows(i)], acc_b[i][u][:, :HALF].rearrange("p (m j) -> p m j", m=2))
        for u in range(2):
            nc.sync.dma_start(out_rows[:, 2 * u : 2 * u + 2, halves[1]], staged_b[u][:])
